import numpy as np
import ml_dtypes


def mxq(x, axis, fmt="e4m3"):
    dtype, down = {"e4m3": (ml_dtypes.float8_e4m3fn, 7), "e5m2": (ml_dtypes.float8_e5m2, 14)}[fmt]
    v = np.moveaxis(np.asarray(x, np.float32).astype(ml_dtypes.bfloat16).astype(np.float64), axis, -1)
    blocks = v.reshape(v.shape[:-1] + (-1, 32))
    amax = np.abs(blocks).max(-1, keepdims=True)
    byte = np.maximum(np.where(amax > 0, np.frexp(amax)[1] - 1 + 127, 0) - down, 1)
    scale = np.exp2(byte - 127.0)
    codes = (blocks / scale).astype(np.float32).astype(dtype).astype(np.float64)
    return np.moveaxis((codes * scale).reshape(v.shape), -1, axis)


WIDE = False


def mx_kscale(k):
    if not WIDE:
        return np.ones(k)
    levels = np.array([10, -10, 5, -5, 0])
    if k % 512:
        return np.exp2(np.random.permutation(np.resize(levels, k // 32))).repeat(32)
    a = np.empty((k // 512, 16))
    for p in range(k // 512):
        a[p, :8] = np.random.permutation(np.resize(levels, 8))
        for g in range(8):
            far = levels[np.abs(levels - a[p, g]) >= 10]
            a[p, g + 8] = far[np.random.randint(len(far))]
    return np.exp2(a.ravel()).repeat(32)


def f64(x):
    return np.asarray(x).astype(np.float64)


def striped(idx):
    return np.tile(idx.reshape(-1, 16).T, (8, 1)).astype(np.uint16)


def unstriped(offs):
    return offs[:16].T.reshape(-1).astype(np.int64)


E2M1 = np.array([0.0, 0.5, 1.0, 1.5, 2.0, 3.0, 4.0, 6.0, -0.0, -0.5, -1.0, -1.5, -2.0, -3.0, -4.0, -6.0])


def pack_weight(w, fmt):
    k, n = w.shape
    w = f64(np.asarray(w, np.float32).astype(ml_dtypes.bfloat16)).reshape(k // 32, 32, n)
    amax = np.abs(w).max(1)
    if fmt == "e4m3":
        byte = np.frexp(amax)[1] - 1 + 127 - 7
    else:
        mant, ex = np.frexp(amax / 6.0)
        byte = np.where(mant > 0.5, ex, ex - 1) + 127
    byte = np.clip(np.where(amax > 0, byte, 1), 1, 254)
    scaled = (w * np.exp2(127.0 - byte)[:, None, :]).reshape(k, n).astype(np.float32)
    by_word = np.ascontiguousarray(scaled.reshape(k // 512, 128, 4, n).transpose(0, 1, 3, 2))
    if fmt == "e4m3":
        words = by_word.astype(ml_dtypes.float8_e4m3fn).view(np.uint8)
    else:
        c = by_word.astype(ml_dtypes.float4_e2m1fn).view(np.uint8) & 0xF
        words = (c[..., 0::2] | (c[..., 1::2] << 4)).reshape(k // 512, 128, 2 * n)
    return np.ascontiguousarray(words), np.ascontiguousarray(byte.astype(np.uint8).reshape(k // 512, 16, n))


def unpack_weight(words, scales, fmt):
    g, _, n = scales.shape
    words = np.ascontiguousarray(words).reshape(g, 128, n, -1)
    if fmt == "e4m3":
        vals = words.view(ml_dtypes.float8_e4m3fn).astype(np.float64)
    else:
        nib = np.empty((g, 128, n, 4), np.uint8)
        nib[..., 0::2] = words & 0xF
        nib[..., 1::2] = words >> 4
        vals = E2M1[nib]
    vals = vals * np.repeat(np.exp2(scales.astype(np.float64) - 127.0), 8, axis=1)[..., None]
    return vals.transpose(0, 1, 3, 2).reshape(g * 512, n)


def relu2(v):
    return np.maximum(v, 0.0) ** 2


K, T, E, C, H, N, HOT = 1024, 640, 10, 128, 512, 128, 5


def by_expert(wq, xq):
    return np.concatenate([wq[e].T @ xq[:, e * C:(e + 1) * C] for e in range(E)], axis=1)


def setup_inputs():
    n = np.random.standard_normal
    s = mx_kscale(K)
    u = mx_kscale(H)
    first = np.random.permutation(np.repeat(np.arange(E), T // E))
    second = (first + 1 + np.random.permutation(np.repeat(np.arange(E - 1), -(-T // (E - 1)))[:T])) % E
    while np.bincount(second, minlength=E).max() != T // E:
        load = np.bincount(second, minlength=E); hi, lo = int(load.argmax()), int(load.argmin())
        t = np.flatnonzero((second == hi) & (first != lo))[0]; second[t] = lo
    slot_token = np.empty(E * C, np.int64); pos = np.empty((2, T), np.int64); fill = np.zeros(E, np.int64)
    place = np.stack([np.random.permutation(C) for _ in range(E)])
    for r, deal in enumerate((first, second)):
        for t in np.random.permutation(T):
            e = deal[t]; j = e * C + place[e, fill[e]]; fill[e] += 1; slot_token[j] = t; pos[r, t] = j
    g = np.random.uniform(0.2, 0.8, T)
    x = pack_weight(n((K, T)) * s[:, None], "e4m3")
    w1h = [pack_weight(m, "e4m3") for m in n((HOT, K, H)) / np.sqrt(K) / s[None, :, None] * u]
    w2h = [pack_weight(m, "e4m3") for m in n((HOT, H, N)) / np.sqrt(H) / u[None, :, None] ** 2]
    w1c = [pack_weight(m, "e2m1") for m in n((E - HOT, K, H)) / np.sqrt(K) / s[None, :, None] * u]
    w2c = [pack_weight(m, "e2m1") for m in n((E - HOT, H, N)) / np.sqrt(H) / u[None, :, None] ** 2]
    return {
        "x_words": x[0],
        "x_scales": x[1],
        "w1h_words": np.stack([m[0] for m in w1h]),
        "w1h_scales": np.stack([m[1] for m in w1h]),
        "w2h_words": np.stack([m[0] for m in w2h]),
        "w2h_scales": np.stack([m[1] for m in w2h]),
        "w1c_words": np.stack([m[0] for m in w1c]),
        "w1c_scales": np.stack([m[1] for m in w1c]),
        "w2c_words": np.stack([m[0] for m in w2c]),
        "w2c_scales": np.stack([m[1] for m in w2c]),
        "gate": np.stack([np.tile(g, (128, 1)), np.tile(1.0 - g, (128, 1))]).astype(np.float32),
        "offs": striped(slot_token),
        "pos1": striped(pos[0]),
        "pos2": striped(pos[1]),
    }


def reference(x_words, x_scales, w1h_words, w1h_scales, w2h_words, w2h_scales, w1c_words, w1c_scales, w2c_words, w2c_scales, gate, offs, pos1, pos2):
    w1h = np.stack([unpack_weight(w1h_words[e], w1h_scales[e], "e4m3") for e in range(HOT)])
    w2h = np.stack([unpack_weight(w2h_words[e], w2h_scales[e], "e4m3") for e in range(HOT)])
    w1c = np.stack([unpack_weight(w1c_words[e], w1c_scales[e], "e2m1") for e in range(E - HOT)])
    w2c = np.stack([unpack_weight(w2c_words[e], w2c_scales[e], "e2m1") for e in range(E - HOT)])
    idx = unstriped(offs)
    xq = unpack_weight(x_words, x_scales, "e4m3")[:, idx]
    w1 = [*w1h, *w1c]
    w2 = [*w2h, *w2c]
    h = relu2(by_expert(w1, xq))
    y = by_expert(w2, mxq(h, 0, "e4m3"))
    out = sum(f64(gate[r, :1]) * y[:, unstriped(p)] for r, p in enumerate((pos1, pos2)))
    return out

@@ -1,0 +1,217 @@
+from contextlib import ExitStack
+
+import concourse.mybir as mybir
+
+K, T, E, C, H, N, HOT = 1024, 640, 10, 128, 512, 128, 5
+COLD = E - HOT
+SLOTS = E * C
+P = 128
+PASSES = K // 512
+FLOPS = 2 * SLOTS * (K * H + H * N)
+
+F32 = mybir.dt.float32
+BF16 = mybir.dt.bfloat16
+I32 = mybir.dt.int32
+U32 = mybir.dt.uint32
+U16 = mybir.dt.uint16
+U8 = mybir.dt.uint8
+FP8X4 = mybir.dt.float8_e4m3fn_x4
+FP4X4 = mybir.dt.float4_e2m1fn_x4
+ACT = mybir.ActivationFunctionType
+ALU = mybir.AluOpType
+
+W1H_ROW = 12
+W2H_ROW = 8
+VECTOR_RELU = (8, 9)
+
+
+def tile_moe_hot_mlp_relu2_kernel(
+    tc, x_words, x_scales, w1h_words, w1h_scales, w2h_words, w2h_scales,
+    w1c_words, w1c_scales, w2c_words, w2c_scales, gate, offs, pos1, pos2, out,
+):
+    nc = tc.nc
+    with ExitStack() as ctx:
+        keep = ctx.enter_context(tc.tile_pool(name="keep", bufs=1))
+        ring = ctx.enter_context(tc.tile_pool(name="ring", bufs=4))
+        psum = ctx.enter_context(tc.psum_pool(name="psum", bufs=1))
+
+        def kept(name, shape, dtype):
+            return keep.tile(shape, dtype, name=name, align_bytes=64)
+
+        offs_t = keep.tile([P, SLOTS // 16], U16, name="offs_t")
+        pos_t = [keep.tile([P, T // 16], U16, name=f"pos_t{r}") for r in range(2)]
+        xw = [kept(f"xw{s}", [P, T], I32) for s in range(PASSES)]
+        xs = kept("xs", [P, T], U8)
+        w1h = [kept(f"w1h{e}", [P, PASSES, H], I32) for e in range(HOT)]
+        w1c = [kept(f"w1c{f}", [P, PASSES, 2 * H], U8) for f in range(COLD)]
+        w2h = kept("w2h", [P, HOT, N], I32)
+        w2c = kept("w2c", [P, COLD, 2 * N], U8)
+        w1hs = kept("w1hs", [P, HOT * PASSES, H], U8)
+        w1cs = kept("w1cs", [P, COLD * PASSES, H], U8)
+        w2hs = kept("w2hs", [P, HOT, N], U8)
+        w2cs = kept("w2cs", [P, COLD, N], U8)
+        gw = [kept(f"gw{s}", [P, SLOTS], U32) for s in range(PASSES)]
+        gs = kept("gs", [P, SLOTS], U8)
+        gs1 = kept("gs1", [P, COLD * C], U8)
+        gates = [kept(f"gate{r}", [P, T], F32) for r in range(2)]
+        y_all = kept("y_all", [P, SLOTS], F32)
+        ident = kept("ident", [P, P], F32)
+
+        h_all = kept("h_all", [P, SLOTS, 4], BF16)
+        h_words = kept("h_words", [P, SLOTS], U32)
+        h_scale = kept("h_scale", [P, SLOTS], U8)
+        ones = kept("ones", [P, 32], F32)
+        column = kept("column", [P, 32], F32)
+        row = kept("row", [P, 32], F32)
+        v_banks = [psum.tile([P, H], F32, name=f"v_bank{i}") for i in range(4)]
+        t_banks = [psum.tile([P, 4, C], F32, name=f"t_bank{i}") for i in range(4)]
+
+        def flat(t):
+            return t[:].rearrange("p a b -> p (a b)")
+
+        def load_scales(queue, plane, first, scales):
+            for q in range(4):
+                queue.dma_start(
+                    plane[32 * q + first : 32 * q + first + 4, :, :].bitcast(I32),
+                    scales[:, :, 4 * q : 4 * q + 4, :].rearrange("e s b i -> b (e s) i").bitcast(I32),
+                )
+
+        nc.gpsimd.memset(xs[:].bitcast(I32), 0)
+        nc.vector.memset(flat(w1hs).bitcast(I32), 0)
+        nc.gpsimd.memset(flat(w1cs).bitcast(I32), 0)
+
+        nc.sync.dma_start(offs_t[:], offs)
+        for q in range(4):
+            nc.scalar.dma_start(xs[32 * q : 32 * q + 8, :].bitcast(I32), x_scales[:, 4 * q : 4 * q + 4, :].bitcast(I32))
+        for s in range(PASSES):
+            nc.sync.dma_start(xw[s][:], x_words[s].rearrange("p t d -> p (t d)").bitcast(I32))
+        load_scales(nc.scalar, w1hs, W1H_ROW, w1h_scales)
+        load_scales(nc.gpsimd, w1cs, 0, w1c_scales)
+        nc.gpsimd.memset(gs1[:].bitcast(I32), 0)
+        nc.gpsimd.memset(flat(w2hs).bitcast(I32), 0)
+        nc.gpsimd.memset(flat(w2cs).bitcast(I32), 0)
+        for e in range(HOT):
+            nc.sync.dma_start(w1h[e][:], w1h_words[e].rearrange("s p i d -> p s (i d)").bitcast(I32))
+        for f in range(COLD):
+            nc.sync.dma_start(w1c[f][:].bitcast(I32), w1c_words[f].rearrange("s p b -> p s b").bitcast(I32))
+        nc.sync.dma_start(w2h[:], w2h_words.rearrange("e s p n d -> p (e s) (n d)").bitcast(I32))
+        load_scales(nc.sync, w2hs, W2H_ROW, w2h_scales)
+        nc.sync.dma_start(w2c[:].bitcast(I32), w2c_words.rearrange("e s p b -> p (e s) b").bitcast(I32))
+        nc.sync.dma_start(gates[0][:], gate[0])
+        load_scales(nc.sync, w2cs, 0, w2c_scales)
+        nc.sync.dma_start(gates[1][:], gate[1])
+        nc.sync.dma_start(pos_t[0][:], pos1)
+        nc.sync.dma_start(pos_t[1][:], pos2)
+
+        nc.vector.memset(ones[:], 1.0)
+        nc.vector.memset(ident[:], 0.0)
+        nc.vector.tensor_tensor_scan(column[:], ones[:], ones[:], 0.0, ALU.mult, ALU.add)
+        nc.vector.transpose(row[:], column[:])
+        for q in range(4):
+            part = slice(32 * q, 32 * q + 32)
+            nc.vector.tensor_tensor(ident[part, part], column[part, :], row[part, :], ALU.is_equal)
+
+        def listed(first, last):
+            return offs_t[:, first * C // 16 : last * C // 16]
+
+        def gather_bytes(first, last):
+            nc.vector.tensor_copy(gs[:, first * C : last * C], xs[:].indirect(listed(first, last)))
+            if first >= HOT:
+                nc.gpsimd.dma_start(
+                    gs1[0:112, (first - HOT) * C : (last - HOT) * C].bitcast(I32),
+                    gs[4:116, first * C : last * C].bitcast(I32),
+                )
+
+        def gather_words(first, last):
+            for s in range(PASSES):
+                nc.vector.tensor_copy(gw[s][:, first * C : last * C], xw[s][:].bitcast(U32).indirect(listed(first, last)))
+
+        gather_bytes(0, 1)
+        gather_words(0, 1)
+        gather_bytes(1, 3)
+        gather_words(1, 2)
+        gather_bytes(5, 7)
+        gather_words(2, 3)
+        gather_bytes(3, 5)
+        gather_words(3, 5)
+        gather_bytes(7, 10)
+        gather_words(5, 7)
+        gather_words(7, 9)
+        gather_words(9, 10)
+
+        def first_layer(e):
+            cols = slice(e * C, (e + 1) * C)
+            v = v_banks[e % 4]
+            for s in range(PASSES):
+                if e < HOT:
+                    x_scale = gs[4 * s : P, cols]
+                    w = w1h[e][:, s, :].bitcast(FP8X4)
+                    w_scale = w1hs[W1H_ROW:P, e * PASSES + s, :]
+                else:
+                    f = e - HOT
+                    x_scale = gs[:, cols] if s == 0 else gs1[:, f * C : (f + 1) * C]
+                    w = w1c[f][:, s, :].bitcast(FP4X4)
+                    w_scale = w1cs[:, f * PASSES + s, :]
+                nc.tensor.matmul_mx(
+                    out=v[:], lhsT=gw[s][:, cols].bitcast(FP8X4), lhsT_scale=x_scale,
+                    rhs=w, rhs_scale=w_scale, start=(s == 0), stop=(s == PASSES - 1),
+                )
+            r = ring.tile([P, 4, P], F32, name="r", align_bytes=64)
+            v_by_t = v[:].rearrange("j (p t) -> j t p", t=4)
+            if e in VECTOR_RELU:
+                nc.vector.tensor_scalar(r[:], v_by_t, 0.0, None, ALU.max)
+            else:
+                nc.scalar.activation(r[:], v_by_t, ACT.Relu)
+            turned = t_banks[e % 4]
+            for t in range(4):
+                nc.tensor.transpose(turned[:, t, :], r[:, t, :], ident[:])
+            nc.scalar.activation(h_all[:, cols, :], turned[:].rearrange("p t j -> p j t"), ACT.Square)
+
+        def quantise(first, last):
+            cols = slice(first * C, last * C)
+            nc.vector.quantize_mx(
+                out=h_words[:, cols].bitcast(FP8X4), scales=h_scale[:, cols],
+                in_=h_all[:, cols, :].rearrange("p j t -> p (j t)"),
+            )
+
+        def second_layer(first, last, bank, copy):
+            for e in range(first, last):
+                cols = slice(e * C, (e + 1) * C)
+                if e < HOT:
+                    w = w2h[:, e, :].bitcast(FP8X4)
+                    w_scale = w2hs[W2H_ROW:P, e, :]
+                else:
+                    w = w2c[:, e - HOT, :].bitcast(FP4X4)
+                    w_scale = w2cs[:, e - HOT, :]
+                nc.tensor.matmul_mx(
+                    out=bank[:, (e - first) * C : (e - first + 1) * C], lhsT=w, lhsT_scale=w_scale,
+                    rhs=h_words[:, cols].bitcast(FP8X4), rhs_scale=h_scale[:, cols], start=True, stop=True,
+                )
+            copy(y_all[:, first * C : last * C], bank[:, 0 : (last - first) * C])
+
+        for e in range(E):
+            first_layer(e)
+        for first, last in ((0, 4), (4, 8), (8, 9), (9, 10)):
+            quantise(first, last)
+        second_layer(0, 4, v_banks[0], nc.vector.tensor_copy)
+        second_layer(4, 8, v_banks[1], nc.scalar.copy)
+        second_layer(8, 10, v_banks[2], nc.scalar.copy)
+
+        HALF = T // 2
+        parts = [[kept(f"part{r}{u}", [P, HALF], F32) for r in range(2)] for u in range(2)]
+        total = [kept(f"total{u}", [P, HALF], F32) for u in range(2)]
+
+        def fetch(u, r):
+            a, b = u * HALF, (u + 1) * HALF
+            nc.vector.tensor_tensor(parts[u][r][:], y_all[:].indirect(pos_t[r][:, a // 16 : b // 16]), gates[r][:, a:b], ALU.mult)
+
+        def finish(u):
+            nc.vector.tensor_tensor(total[u][:], parts[u][0][:], parts[u][1][:], ALU.add)
+            nc.sync.dma_start(out[:, u * HALF : (u + 1) * HALF], total[u][:])
+
+        fetch(0, 0)
+        fetch(0, 1)
+        fetch(1, 0)
+        finish(0)
+        fetch(1, 1)
+        finish(1)

@@ -43,28 +43,25 @@ def tile_moe_hot_mlp_relu2_kernel(
         xw = [kept(f"xw{s}", [P, T], I32) for s in range(PASSES)]
         xs = kept("xs", [P, T], U8)
         w1h = [kept(f"w1h{e}", [P, PASSES, H], I32) for e in range(HOT)]
-        w1c = [kept(f"w1c{f}", [P, PASSES, 2 * H], U8) for f in range(COLD)]
+        w1c = kept("w1c", [P, COLD * PASSES, 2 * H], U8)
         w2h = kept("w2h", [P, HOT, N], I32)
         w2c = kept("w2c", [P, COLD, 2 * N], U8)
         w1hs = kept("w1hs", [P, HOT * PASSES, H], U8)
-        w1cs = kept("w1cs", [P, COLD * PASSES, H], U8)
-        w2hs = kept("w2hs", [P, HOT, N], U8)
-        w2cs = kept("w2cs", [P, COLD, N], U8)
         gw = [kept(f"gw{s}", [P, SLOTS], U32) for s in range(PASSES)]
         gs = kept("gs", [P, SLOTS], U8)
-        gs1 = kept("gs1", [P, COLD * C], U8)
-        gates = [kept(f"gate{r}", [P, T], F32) for r in range(2)]
+        gates = kept("gates", [P, 2, T], F32)
         y_all = kept("y_all", [P, SLOTS], F32)
         ident = kept("ident", [P, P], F32)
 
         h_all = kept("h_all", [P, SLOTS, 4], BF16)
         h_words = kept("h_words", [P, SLOTS], U32)
         h_scale = kept("h_scale", [P, SLOTS], U8)
-        ones = kept("ones", [P, 32], F32)
+        ones = keep.tile([P, 32], F32, name="ones", tag="first", align_bytes=64)
         column = kept("column", [P, 32], F32)
-        row = kept("row", [P, 32], F32)
-        v_banks = [psum.tile([P, H], F32, name=f"v_bank{i}") for i in range(4)]
-        t_banks = [psum.tile([P, 4, C], F32, name=f"t_bank{i}") for i in range(4)]
+        row = keep.tile([P, 32], F32, name="row", tag="second", align_bytes=64)
+        v_banks = [psum.tile([P, H], F32, name=f"v_bank{i}") for i in range(3)]
+        t_banks = [psum.tile([P, 4, C], F32, name=f"t_bank{i}") for i in range(2)]
+        last_bank = psum.tile([P, 2 * C], F32, name="last_bank")
 
         def flat(t):
             return t[:].rearrange("p a b -> p (a b)")
@@ -76,32 +73,29 @@ def tile_moe_hot_mlp_relu2_kernel(
                     scales[:, :, 4 * q : 4 * q + 4, :].rearrange("e s b i -> b (e s) i").bitcast(I32),
                 )
 
-        nc.gpsimd.memset(xs[:].bitcast(I32), 0)
-        nc.vector.memset(flat(w1hs).bitcast(I32), 0)
-        nc.gpsimd.memset(flat(w1cs).bitcast(I32), 0)
+        def load_w1h(queue, e):
+            queue.dma_start(w1h[e][:], w1h_words[e].rearrange("s p i d -> p s (i d)").bitcast(I32))
 
-        nc.sync.dma_start(offs_t[:], offs)
-        for q in range(4):
-            nc.scalar.dma_start(xs[32 * q : 32 * q + 8, :].bitcast(I32), x_scales[:, 4 * q : 4 * q + 4, :].bitcast(I32))
-        for s in range(PASSES):
+        def load_w1c(f):
+            nc.sync.dma_start(w1c[:, f * PASSES : (f + 1) * PASSES, :].bitcast(I32), w1c_words[f].rearrange("s p b -> p s b").bitcast(I32))
+
+        def load_x(s):
             nc.sync.dma_start(xw[s][:], x_words[s].rearrange("p t d -> p (t d)").bitcast(I32))
-        load_scales(nc.scalar, w1hs, W1H_ROW, w1h_scales)
-        load_scales(nc.gpsimd, w1cs, 0, w1c_scales)
-        nc.gpsimd.memset(gs1[:].bitcast(I32), 0)
-        nc.gpsimd.memset(flat(w2hs).bitcast(I32), 0)
-        nc.gpsimd.memset(flat(w2cs).bitcast(I32), 0)
-        for e in range(HOT):
-            nc.sync.dma_start(w1h[e][:], w1h_words[e].rearrange("s p i d -> p s (i d)").bitcast(I32))
-        for f in range(COLD):
-            nc.sync.dma_start(w1c[f][:].bitcast(I32), w1c_words[f].rearrange("s p b -> p s b").bitcast(I32))
-        nc.sync.dma_start(w2h[:], w2h_words.rearrange("e s p n d -> p (e s) (n d)").bitcast(I32))
-        load_scales(nc.sync, w2hs, W2H_ROW, w2h_scales)
-        nc.sync.dma_start(w2c[:].bitcast(I32), w2c_words.rearrange("e s p b -> p (e s) b").bitcast(I32))
-        nc.sync.dma_start(gates[0][:], gate[0])
-        load_scales(nc.sync, w2cs, 0, w2c_scales)
-        nc.sync.dma_start(gates[1][:], gate[1])
-        nc.sync.dma_start(pos_t[0][:], pos1)
-        nc.sync.dma_start(pos_t[1][:], pos2)
+
+        nc.vector.memset(xs[:].bitcast(I32), 0)
+        nc.vector.memset(flat(w1hs).bitcast(I32), 0)
+
+        load_x(0)
+        for q in range(4):
+            nc.sync.dma_start(xs[32 * q : 32 * q + 8, :].bitcast(I32), x_scales[:, 4 * q : 4 * q + 4, :].bitcast(I32))
+        load_x(1)
+        nc.sync.dma_start(offs_t[:], offs)
+        load_w1h(nc.sync, 0)
+        load_scales(nc.sync, w1hs, W1H_ROW, w1h_scales)
+        load_w1h(nc.sync, 1)
+        load_w1h(nc.sync, 2)
+        load_w1h(nc.sync, 3)
+        load_w1h(nc.sync, 4)
 
         nc.vector.memset(ones[:], 1.0)
         nc.vector.memset(ident[:], 0.0)
@@ -111,13 +105,23 @@ def tile_moe_hot_mlp_relu2_kernel(
             part = slice(32 * q, 32 * q + 32)
             nc.vector.tensor_tensor(ident[part, part], column[part, :], row[part, :], ALU.is_equal)
 
+        gs1 = keep.tile([P, COLD * C], U8, name="gs1", tag="first", align_bytes=64)
+        late = keep.tile([P, COLD * PASSES * H + E * N], U8, name="late", tag="second", align_bytes=64)
+        w1cs = late[:, 0 : COLD * PASSES * H].rearrange("p (a i) -> p a i", i=H)
+        w2s = late[:, COLD * PASSES * H :].rearrange("p (e n) -> p e n", n=N)
+        w2hs = w2s[:, 0:HOT, :]
+        w2cs = w2s[:, HOT:E, :]
+        nc.gpsimd.memset(gs1[:].bitcast(I32), 0)
+        nc.gpsimd.memset(late[:, 0 : COLD * PASSES * H].bitcast(I32), 0)
+        nc.gpsimd.memset(late[:, COLD * PASSES * H :].bitcast(I32), 0)
+
         def listed(first, last):
             return offs_t[:, first * C // 16 : last * C // 16]
 
         def gather_bytes(first, last):
             nc.vector.tensor_copy(gs[:, first * C : last * C], xs[:].indirect(listed(first, last)))
             if first >= HOT:
-                nc.gpsimd.dma_start(
+                nc.sync.dma_start(
                     gs1[0:112, (first - HOT) * C : (last - HOT) * C].bitcast(I32),
                     gs[4:116, first * C : last * C].bitcast(I32),
                 )
@@ -131,17 +135,33 @@ def tile_moe_hot_mlp_relu2_kernel(
         gather_bytes(1, 3)
         gather_words(1, 2)
         gather_bytes(5, 7)
+        load_scales(nc.sync, w1cs, 0, w1c_scales)
+        for f in range(3):
+            load_w1c(f)
         gather_words(2, 3)
         gather_bytes(3, 5)
-        gather_words(3, 5)
+        gather_words(3, 4)
+        gather_words(4, 5)
         gather_bytes(7, 10)
-        gather_words(5, 7)
+        load_w1c(3)
+        load_w1c(4)
+        nc.sync.dma_start(w2h[:], w2h_words.rearrange("e s p n d -> p (e s) (n d)").bitcast(I32))
+        nc.sync.dma_start(w2c[:].bitcast(I32), w2c_words.rearrange("e s p b -> p (e s) b").bitcast(I32))
+        load_scales(nc.sync, w2hs, W2H_ROW, w2h_scales)
+        load_scales(nc.sync, w2cs, 0, w2c_scales)
+        nc.sync.dma_start(pos_t[0][:], pos1)
+        nc.sync.dma_start(pos_t[1][:], pos2)
+        nc.sync.dma_start(gates[:], gate.rearrange("r p t -> p r t"))
+
+        gather_words(5, 6)
+        gather_words(6, 7)
         gather_words(7, 9)
         gather_words(9, 10)
 
+
         def first_layer(e):
             cols = slice(e * C, (e + 1) * C)
-            v = v_banks[e % 4]
+            v = v_banks[e % 3]
             for s in range(PASSES):
                 if e < HOT:
                     x_scale = gs[4 * s : P, cols]
@@ -150,21 +170,32 @@ def tile_moe_hot_mlp_relu2_kernel(
                 else:
                     f = e - HOT
                     x_scale = gs[:, cols] if s == 0 else gs1[:, f * C : (f + 1) * C]
-                    w = w1c[f][:, s, :].bitcast(FP4X4)
+                    w = w1c[:, f * PASSES + s, :].bitcast(FP4X4)
                     w_scale = w1cs[:, f * PASSES + s, :]
                 nc.tensor.matmul_mx(
                     out=v[:], lhsT=gw[s][:, cols].bitcast(FP8X4), lhsT_scale=x_scale,
                     rhs=w, rhs_scale=w_scale, start=(s == 0), stop=(s == PASSES - 1),
                 )
+
+        relus = {}
+
+        def relu(e):
+            v = v_banks[e % 3]
             r = ring.tile([P, 4, P], F32, name="r", align_bytes=64)
+            relus[e] = r
             v_by_t = v[:].rearrange("j (p t) -> j t p", t=4)
             if e in VECTOR_RELU:
                 nc.vector.tensor_scalar(r[:], v_by_t, 0.0, None, ALU.max)
             else:
                 nc.scalar.activation(r[:], v_by_t, ACT.Relu)
-            turned = t_banks[e % 4]
+
+        def turn(e):
             for t in range(4):
-                nc.tensor.transpose(turned[:, t, :], r[:, t, :], ident[:])
+                nc.tensor.transpose(t_banks[e % 2][:, t, :], relus[e][:, t, :], ident[:])
+
+        def square(e):
+            cols = slice(e * C, (e + 1) * C)
+            turned = t_banks[e % 2]
             nc.scalar.activation(h_all[:, cols, :], turned[:].rearrange("p t j -> p j t"), ACT.Square)
 
         def quantise(first, last):
@@ -189,13 +220,21 @@ def tile_moe_hot_mlp_relu2_kernel(
                 )
             copy(y_all[:, first * C : last * C], bank[:, 0 : (last - first) * C])
 
+        first_layer(0)
+        first_layer(1)
+        relu(0)
         for e in range(E):
-            first_layer(e)
+            turn(e)
+            if e + 2 < E:
+                first_layer(e + 2)
+            if e + 1 < E:
+                relu(e + 1)
+            square(e)
         for first, last in ((0, 4), (4, 8), (8, 9), (9, 10)):
             quantise(first, last)
-        second_layer(0, 4, v_banks[0], nc.vector.tensor_copy)
-        second_layer(4, 8, v_banks[1], nc.scalar.copy)
-        second_layer(8, 10, v_banks[2], nc.scalar.copy)
+        second_layer(0, 4, v_banks[2], nc.vector.tensor_copy)
+        second_layer(4, 8, v_banks[0], nc.scalar.copy)
+        second_layer(8, 10, last_bank, nc.scalar.copy)
 
         HALF = T // 2
         parts = [[kept(f"part{r}{u}", [P, HALF], F32) for r in range(2)] for u in range(2)]
@@ -203,7 +242,7 @@ def tile_moe_hot_mlp_relu2_kernel(
 
         def fetch(u, r):
             a, b = u * HALF, (u + 1) * HALF
-            nc.vector.tensor_tensor(parts[u][r][:], y_all[:].indirect(pos_t[r][:, a // 16 : b // 16]), gates[r][:, a:b], ALU.mult)
+            nc.vector.tensor_tensor(parts[u][r][:], y_all[:].indirect(pos_t[r][:, a // 16 : b // 16]), gates[:, r, a:b], ALU.mult)
 
         def finish(u):
             nc.vector.tensor_tensor(total[u][:], parts[u][0][:], parts[u][1][:], ALU.add)

@@ -20,6 +20,7 @@ FP4X4 = mybir.dt.float4_e2m1fn_x4
 ACT = mybir.ActivationFunctionType
 ALU = mybir.AluOpType
 
+ORDER = (5, 6, 7, 8, 9, 0, 1, 2, 3, 4)
 W1H_ROW = 12
 W2H_ROW = 8
 VECTOR_RELU = (8, 9)
@@ -41,162 +42,149 @@ def tile_moe_hot_mlp_relu2_kernel(
         offs_t = keep.tile([P, SLOTS // 16], U16, name="offs_t")
         pos_t = [keep.tile([P, T // 16], U16, name=f"pos_t{r}") for r in range(2)]
         xw = [kept(f"xw{s}", [P, T], I32) for s in range(PASSES)]
-        xs = kept("xs", [P, T], U8)
+        xs_cold_tile = kept("xs_cold", [P, PASSES * T + 4], U8)
+        xs_cold = xs_cold_tile[:, 0 : PASSES * T].rearrange("p (s t) -> p s t", s=PASSES)
+        xs_hot = kept("xs_hot", [P, T], U8)
         w1h = [kept(f"w1h{e}", [P, PASSES, H], I32) for e in range(HOT)]
-        w1c = kept("w1c", [P, COLD * PASSES, 2 * H], U8)
+        w1c = [kept(f"w1c{f}", [P, PASSES, 2 * H], U8) for f in range(COLD)]
         w2h = kept("w2h", [P, HOT, N], I32)
         w2c = kept("w2c", [P, COLD, 2 * N], U8)
         w1hs = kept("w1hs", [P, HOT * PASSES, H], U8)
+        w1cs_tile = kept("w1cs", [P, COLD * PASSES * H + 4], U8)
+        w1cs = w1cs_tile[:, 0 : COLD * PASSES * H].rearrange("p (a i) -> p a i", i=H)
+        w2s = kept("w2s", [P, E, N], U8)
         gw = [kept(f"gw{s}", [P, SLOTS], U32) for s in range(PASSES)]
-        gs = kept("gs", [P, SLOTS], U8)
+        gs_cold = [kept(f"gs_cold{s}", [P, COLD * C], U8) for s in range(PASSES)]
+        gs_hot = kept("gs_hot", [P, HOT * C], U8)
         gates = kept("gates", [P, 2, T], F32)
         y_all = kept("y_all", [P, SLOTS], F32)
         ident = kept("ident", [P, P], F32)
-
         h_all = kept("h_all", [P, SLOTS, 4], BF16)
         h_words = kept("h_words", [P, SLOTS], U32)
         h_scale = kept("h_scale", [P, SLOTS], U8)
-        ones = keep.tile([P, 32], F32, name="ones", tag="first", align_bytes=64)
+        ones = kept("ones", [P, 32], F32)
         column = kept("column", [P, 32], F32)
-        row = keep.tile([P, 32], F32, name="row", tag="second", align_bytes=64)
+        row = kept("row", [P, 32], F32)
         v_banks = [psum.tile([P, H], F32, name=f"v_bank{i}") for i in range(3)]
         t_banks = [psum.tile([P, 4, C], F32, name=f"t_bank{i}") for i in range(2)]
         last_bank = psum.tile([P, 2 * C], F32, name="last_bank")
 
-        def flat(t):
-            return t[:].rearrange("p a b -> p (a b)")
+        def zero(plane):
+            nc.gpsimd.memset(plane[:].rearrange("p a b -> p (a b)").bitcast(I32), 0)
 
-        def load_scales(queue, plane, first, scales):
-            for q in range(4):
-                queue.dma_start(
-                    plane[32 * q + first : 32 * q + first + 4, :, :].bitcast(I32),
-                    scales[:, :, 4 * q : 4 * q + 4, :].rearrange("e s b i -> b (e s) i").bitcast(I32),
+        def load_scales(plane, first, scales):
+            for r in range(4):
+                nc.sync.dma_start(
+                    plane[first + r : P : 32, :, :].bitcast(I32),
+                    scales[:, :, r:16:4, :].rearrange("e s q i -> q (e s) i").bitcast(I32),
                 )
-
-        def load_w1h(queue, e):
-            queue.dma_start(w1h[e][:], w1h_words[e].rearrange("s p i d -> p s (i d)").bitcast(I32))
-
-        def load_w1c(f):
-            nc.sync.dma_start(w1c[:, f * PASSES : (f + 1) * PASSES, :].bitcast(I32), w1c_words[f].rearrange("s p b -> p s b").bitcast(I32))
 
         def load_x(s):
             nc.sync.dma_start(xw[s][:], x_words[s].rearrange("p t d -> p (t d)").bitcast(I32))
 
-        nc.vector.memset(xs[:].bitcast(I32), 0)
-        nc.vector.memset(flat(w1hs).bitcast(I32), 0)
+        def load_w1h(e):
+            nc.sync.dma_start(w1h[e][:], w1h_words[e].rearrange("s p i d -> p s (i d)").bitcast(I32))
 
-        load_x(0)
-        for q in range(4):
-            nc.sync.dma_start(xs[32 * q : 32 * q + 8, :].bitcast(I32), x_scales[:, 4 * q : 4 * q + 4, :].bitcast(I32))
-        load_x(1)
-        nc.sync.dma_start(offs_t[:], offs)
-        load_w1h(nc.sync, 0)
-        load_scales(nc.sync, w1hs, W1H_ROW, w1h_scales)
-        load_w1h(nc.sync, 1)
-        load_w1h(nc.sync, 2)
-        load_w1h(nc.sync, 3)
-        load_w1h(nc.sync, 4)
+        def load_w1c(f):
+            nc.sync.dma_start(w1c[f][:].bitcast(I32), w1c_words[f].rearrange("s p b -> p s b").bitcast(I32))
 
-        nc.vector.memset(ones[:], 1.0)
-        nc.vector.memset(ident[:], 0.0)
+        nc.vector.memset(xs_cold_tile[:, 0 : PASSES * T + 4].bitcast(I32), 0)
+        nc.vector.memset(w1cs_tile[:, 0 : COLD * PASSES * H + 4].bitcast(I32), 0)
+        nc.gpsimd.memset(ones[:], 1.0)
+        nc.gpsimd.memset(ident[:], 0.0)
+        nc.gpsimd.memset(xs_hot[:].bitcast(I32), 0)
+        zero(w1hs)
+        zero(w2s)
         nc.vector.tensor_tensor_scan(column[:], ones[:], ones[:], 0.0, ALU.mult, ALU.add)
         nc.vector.transpose(row[:], column[:])
         for q in range(4):
             part = slice(32 * q, 32 * q + 32)
             nc.vector.tensor_tensor(ident[part, part], column[part, :], row[part, :], ALU.is_equal)
 
-        gs1 = keep.tile([P, COLD * C], U8, name="gs1", tag="first", align_bytes=64)
-        late = keep.tile([P, COLD * PASSES * H + E * N], U8, name="late", tag="second", align_bytes=64)
-        w1cs = late[:, 0 : COLD * PASSES * H].rearrange("p (a i) -> p a i", i=H)
-        w2s = late[:, COLD * PASSES * H :].rearrange("p (e n) -> p e n", n=N)
-        w2hs = w2s[:, 0:HOT, :]
-        w2cs = w2s[:, HOT:E, :]
-        nc.gpsimd.memset(gs1[:].bitcast(I32), 0)
-        nc.gpsimd.memset(late[:, 0 : COLD * PASSES * H].bitcast(I32), 0)
-        nc.gpsimd.memset(late[:, COLD * PASSES * H :].bitcast(I32), 0)
+        load_x(0)
+        for r in range(4):
+            nc.sync.dma_start(xs_cold[r:P:32, :, :].bitcast(I32), x_scales[:, r:16:4, :].rearrange("s q t -> q s t").bitcast(I32))
+        load_x(1)
+        nc.sync.dma_start(offs_t[:], offs)
+        load_w1c(0)
+        load_scales(w1cs, 0, w1c_scales)
+        load_w1c(1)
+        load_w1c(2)
+        for q in range(4):
+            nc.sync.dma_start(xs_hot[32 * q : 32 * q + 8, :].bitcast(I32), x_scales[:, 4 * q : 4 * q + 4, :].bitcast(I32))
+        load_w1c(3)
+        load_w1c(4)
+        load_w1h(0)
+        load_scales(w1hs, W1H_ROW, w1h_scales)
+        for e in range(1, HOT):
+            load_w1h(e)
+        nc.sync.dma_start(w2c[:].bitcast(I32), w2c_words.rearrange("e s p b -> p (e s) b").bitcast(I32))
+        load_scales(w2s[:, HOT:E, :], 0, w2c_scales)
+        nc.sync.dma_start(w2h[:], w2h_words.rearrange("e s p n d -> p (e s) (n d)").bitcast(I32))
+        load_scales(w2s[:, 0:HOT, :], W2H_ROW, w2h_scales)
+        nc.sync.dma_start(gates[:], gate.rearrange("r p t -> p r t"))
+        nc.sync.dma_start(pos_t[0][:], pos1)
+        nc.sync.dma_start(pos_t[1][:], pos2)
 
         def listed(first, last):
             return offs_t[:, first * C // 16 : last * C // 16]
 
         def gather_bytes(first, last):
-            nc.vector.tensor_copy(gs[:, first * C : last * C], xs[:].indirect(listed(first, last)))
-            if first >= HOT:
-                nc.sync.dma_start(
-                    gs1[0:112, (first - HOT) * C : (last - HOT) * C].bitcast(I32),
-                    gs[4:116, first * C : last * C].bitcast(I32),
-                )
+            if first < HOT:
+                nc.vector.tensor_copy(gs_hot[:, first * C : last * C], xs_hot[:].indirect(listed(first, last)))
+            else:
+                for s in range(PASSES):
+                    nc.vector.tensor_copy(
+                        gs_cold[s][:, (first - HOT) * C : (last - HOT) * C], xs_cold[:, s, :].indirect(listed(first, last))
+                    )
 
         def gather_words(first, last):
             for s in range(PASSES):
                 nc.vector.tensor_copy(gw[s][:, first * C : last * C], xw[s][:].bitcast(U32).indirect(listed(first, last)))
 
-        gather_bytes(0, 1)
-        gather_words(0, 1)
-        gather_bytes(1, 3)
-        gather_words(1, 2)
-        gather_bytes(5, 7)
-        load_scales(nc.sync, w1cs, 0, w1c_scales)
-        for f in range(3):
-            load_w1c(f)
-        gather_words(2, 3)
-        gather_bytes(3, 5)
-        gather_words(3, 4)
-        gather_words(4, 5)
-        gather_bytes(7, 10)
-        load_w1c(3)
-        load_w1c(4)
-        nc.sync.dma_start(w2h[:], w2h_words.rearrange("e s p n d -> p (e s) (n d)").bitcast(I32))
-        nc.sync.dma_start(w2c[:].bitcast(I32), w2c_words.rearrange("e s p b -> p (e s) b").bitcast(I32))
-        load_scales(nc.sync, w2hs, W2H_ROW, w2h_scales)
-        load_scales(nc.sync, w2cs, 0, w2c_scales)
-        nc.sync.dma_start(pos_t[0][:], pos1)
-        nc.sync.dma_start(pos_t[1][:], pos2)
-        nc.sync.dma_start(gates[:], gate.rearrange("r p t -> p r t"))
+        for first, last in ((5, 8), (8, 10)):
+            gather_bytes(first, last)
+            gather_words(first, last)
+        for first, last in ((0, 2), (2, 5)):
+            gather_bytes(first, last)
+            for e in range(first, last):
+                gather_words(e, e + 1)
 
-        gather_words(5, 6)
-        gather_words(6, 7)
-        gather_words(7, 9)
-        gather_words(9, 10)
+        relus = {}
 
-
-        def first_layer(e):
+        def first_layer(j):
+            e = ORDER[j]
             cols = slice(e * C, (e + 1) * C)
-            v = v_banks[e % 3]
             for s in range(PASSES):
                 if e < HOT:
-                    x_scale = gs[4 * s : P, cols]
+                    x_scale = gs_hot[4 * s : P, cols]
                     w = w1h[e][:, s, :].bitcast(FP8X4)
                     w_scale = w1hs[W1H_ROW:P, e * PASSES + s, :]
                 else:
                     f = e - HOT
-                    x_scale = gs[:, cols] if s == 0 else gs1[:, f * C : (f + 1) * C]
-                    w = w1c[:, f * PASSES + s, :].bitcast(FP4X4)
+                    x_scale = gs_cold[s][:, f * C : (f + 1) * C]
+                    w = w1c[f][:, s, :].bitcast(FP4X4)
                     w_scale = w1cs[:, f * PASSES + s, :]
                 nc.tensor.matmul_mx(
-                    out=v[:], lhsT=gw[s][:, cols].bitcast(FP8X4), lhsT_scale=x_scale,
+                    out=v_banks[j % 3][:], lhsT=gw[s][:, cols].bitcast(FP8X4), lhsT_scale=x_scale,
                     rhs=w, rhs_scale=w_scale, start=(s == 0), stop=(s == PASSES - 1),
                 )
 
-        relus = {}
-
-        def relu(e):
-            v = v_banks[e % 3]
+        def relu(j):
             r = ring.tile([P, 4, P], F32, name="r", align_bytes=64)
-            relus[e] = r
-            v_by_t = v[:].rearrange("j (p t) -> j t p", t=4)
-            if e in VECTOR_RELU:
+            relus[j] = r
+            v_by_t = v_banks[j % 3][:].rearrange("j (p t) -> j t p", t=4)
+            if j in VECTOR_RELU:
                 nc.vector.tensor_scalar(r[:], v_by_t, 0.0, None, ALU.max)
             else:
                 nc.scalar.activation(r[:], v_by_t, ACT.Relu)
 
-        def turn(e):
+        def turn(j):
             for t in range(4):
-                nc.tensor.transpose(t_banks[e % 2][:, t, :], relus[e][:, t, :], ident[:])
+                nc.tensor.transpose(t_banks[j % 2][:, t, :], relus[j][:, t, :], ident[:])
 
-        def square(e):
-            cols = slice(e * C, (e + 1) * C)
-            turned = t_banks[e % 2]
-            nc.scalar.activation(h_all[:, cols, :], turned[:].rearrange("p t j -> p j t"), ACT.Square)
+        def square(j):
+            nc.scalar.activation(h_all[:, j * C : (j + 1) * C, :], t_banks[j % 2][:].rearrange("p t j -> p j t"), ACT.Square)
 
         def quantise(first, last):
             cols = slice(first * C, last * C)
@@ -205,36 +193,42 @@ def tile_moe_hot_mlp_relu2_kernel(
                 in_=h_all[:, cols, :].rearrange("p j t -> p (j t)"),
             )
 
-        def second_layer(first, last, bank, copy):
-            for e in range(first, last):
-                cols = slice(e * C, (e + 1) * C)
-                if e < HOT:
-                    w = w2h[:, e, :].bitcast(FP8X4)
-                    w_scale = w2hs[W2H_ROW:P, e, :]
-                else:
-                    w = w2c[:, e - HOT, :].bitcast(FP4X4)
-                    w_scale = w2cs[:, e - HOT, :]
-                nc.tensor.matmul_mx(
-                    out=bank[:, (e - first) * C : (e - first + 1) * C], lhsT=w, lhsT_scale=w_scale,
-                    rhs=h_words[:, cols].bitcast(FP8X4), rhs_scale=h_scale[:, cols], start=True, stop=True,
-                )
-            copy(y_all[:, first * C : last * C], bank[:, 0 : (last - first) * C])
+        def second_layer(j, bank, place):
+            e = ORDER[j]
+            cols = slice(j * C, (j + 1) * C)
+            if e < HOT:
+                w = w2h[:, e, :].bitcast(FP8X4)
+                w_scale = w2s[W2H_ROW:P, e, :]
+            else:
+                w = w2c[:, e - HOT, :].bitcast(FP4X4)
+                w_scale = w2s[:, e, :]
+            nc.tensor.matmul_mx(
+                out=bank[:, place * C : (place + 1) * C], lhsT=w, lhsT_scale=w_scale,
+                rhs=h_words[:, cols].bitcast(FP8X4), rhs_scale=h_scale[:, cols], start=True, stop=True,
+            )
 
         first_layer(0)
         first_layer(1)
         relu(0)
-        for e in range(E):
-            turn(e)
-            if e + 2 < E:
-                first_layer(e + 2)
-            if e + 1 < E:
-                relu(e + 1)
-            square(e)
+        for j in range(E):
+            turn(j)
+            if j + 2 < E:
+                first_layer(j + 2)
+            if j + 1 < E:
+                relu(j + 1)
+            square(j)
         for first, last in ((0, 4), (4, 8), (8, 9), (9, 10)):
             quantise(first, last)
-        second_layer(0, 4, v_banks[2], nc.vector.tensor_copy)
-        second_layer(4, 8, v_banks[0], nc.scalar.copy)
-        second_layer(8, 10, last_bank, nc.scalar.copy)
+        for j in range(4):
+            second_layer(j, v_banks[2], j)
+        nc.vector.tensor_copy(y_all[:, 5 * C : 9 * C], v_banks[2][:])
+        for j in range(4, 8):
+            second_layer(j, v_banks[0], j - 4)
+        nc.scalar.copy(y_all[:, 9 * C : 10 * C], v_banks[0][:, 0:C])
+        nc.scalar.copy(y_all[:, 0 : 3 * C], v_banks[0][:, C : 4 * C])
+        for j in range(8, 10):
+            second_layer(j, last_bank, j - 8)
+        nc.scalar.copy(y_all[:, 3 * C : 5 * C], last_bank[:])
 
         HALF = T // 2
         parts = [[kept(f"part{r}{u}", [P, HALF], F32) for r in range(2)] for u in range(2)]

@@ -20,10 +20,10 @@ FP4X4 = mybir.dt.float4_e2m1fn_x4
 ACT = mybir.ActivationFunctionType
 ALU = mybir.AluOpType
 
-ORDER = (5, 6, 7, 8, 9, 0, 1, 2, 3, 4)
+ORDER = (6, 7, 8, 9, 5, 4, 2, 3, 0, 1)
 W1H_ROW = 12
 W2H_ROW = 8
-VECTOR_RELU = (8, 9)
+VECTOR_RELU = (7, 8, 9)
 
 
 def tile_moe_hot_mlp_relu2_kernel(
@@ -39,89 +39,81 @@ def tile_moe_hot_mlp_relu2_kernel(
         def kept(name, shape, dtype):
             return keep.tile(shape, dtype, name=name, align_bytes=64)
 
+        def after(tag, name, shape, dtype):
+            return keep.tile(shape, dtype, name=name, tag=tag, align_bytes=64)
+
         offs_t = keep.tile([P, SLOTS // 16], U16, name="offs_t")
         pos_t = [keep.tile([P, T // 16], U16, name=f"pos_t{r}") for r in range(2)]
-        xw = [kept(f"xw{s}", [P, T], I32) for s in range(PASSES)]
+        xw = kept("xw", [P, PASSES, T], I32)
         xs_cold_tile = kept("xs_cold", [P, PASSES * T + 4], U8)
         xs_cold = xs_cold_tile[:, 0 : PASSES * T].rearrange("p (s t) -> p s t", s=PASSES)
         xs_hot = kept("xs_hot", [P, T], U8)
         w1h = [kept(f"w1h{e}", [P, PASSES, H], I32) for e in range(HOT)]
-        w1c = [kept(f"w1c{f}", [P, PASSES, 2 * H], U8) for f in range(COLD)]
+        w1c_head = [after(f"head{u}", f"w1c_head{u}", [P, PASSES, 2 * H], U8) for u in range(2)]
+        w1c_next = after("next", "w1c_next", [P, 2 * PASSES, 2 * H], U8)
+        w1c_last = kept("w1c_last", [P, PASSES, 2 * H], U8)
         w2h = kept("w2h", [P, HOT, N], I32)
         w2c = kept("w2c", [P, COLD, 2 * N], U8)
         w1hs = kept("w1hs", [P, HOT * PASSES, H], U8)
-        w1cs_tile = kept("w1cs", [P, COLD * PASSES * H + 4], U8)
-        w1cs = w1cs_tile[:, 0 : COLD * PASSES * H].rearrange("p (a i) -> p a i", i=H)
+        w1cs = kept("w1cs", [P, COLD * PASSES, H], U8)
         w2s = kept("w2s", [P, E, N], U8)
-        gw = [kept(f"gw{s}", [P, SLOTS], U32) for s in range(PASSES)]
-        gs_cold = [kept(f"gs_cold{s}", [P, COLD * C], U8) for s in range(PASSES)]
-        gs_hot = kept("gs_hot", [P, HOT * C], U8)
         gates = kept("gates", [P, 2, T], F32)
         y_all = kept("y_all", [P, SLOTS], F32)
         ident = kept("ident", [P, P], F32)
         h_all = kept("h_all", [P, SLOTS, 4], BF16)
         h_words = kept("h_words", [P, SLOTS], U32)
         h_scale = kept("h_scale", [P, SLOTS], U8)
-        ones = kept("ones", [P, 32], F32)
+        ones = kept("ones", [P, P], F32)
         column = kept("column", [P, 32], F32)
         row = kept("row", [P, 32], F32)
-        v_banks = [psum.tile([P, H], F32, name=f"v_bank{i}") for i in range(3)]
-        t_banks = [psum.tile([P, 4, C], F32, name=f"t_bank{i}") for i in range(2)]
-        last_bank = psum.tile([P, 2 * C], F32, name="last_bank")
+        banks = [psum.tile([P, H], F32, name=f"bank{i}") for i in range(8)]
+        v_bank = [banks[j % 2] for j in range(E)]
+        t_bank = [banks[i] for i in (2, 3, 2, 3, 2, 5, 2, 3, 2, 4)]
 
         def zero(plane):
             nc.gpsimd.memset(plane[:].rearrange("p a b -> p (a b)").bitcast(I32), 0)
 
-        def load_scales(plane, first, scales):
+        def load_scales(queue, plane, first, scales):
             for r in range(4):
-                nc.sync.dma_start(
+                queue.dma_start(
                     plane[first + r : P : 32, :, :].bitcast(I32),
                     scales[:, :, r:16:4, :].rearrange("e s q i -> q (e s) i").bitcast(I32),
                 )
 
-        def load_x(s):
-            nc.sync.dma_start(xw[s][:], x_words[s].rearrange("p t d -> p (t d)").bitcast(I32))
-
         def load_w1h(e):
             nc.sync.dma_start(w1h[e][:], w1h_words[e].rearrange("s p i d -> p s (i d)").bitcast(I32))
 
-        def load_w1c(f):
-            nc.sync.dma_start(w1c[f][:].bitcast(I32), w1c_words[f].rearrange("s p b -> p s b").bitcast(I32))
-
         nc.vector.memset(xs_cold_tile[:, 0 : PASSES * T + 4].bitcast(I32), 0)
-        nc.vector.memset(w1cs_tile[:, 0 : COLD * PASSES * H + 4].bitcast(I32), 0)
         nc.gpsimd.memset(ones[:], 1.0)
-        nc.gpsimd.memset(ident[:], 0.0)
-        nc.gpsimd.memset(xs_hot[:].bitcast(I32), 0)
-        zero(w1hs)
+        nc.scalar.activation(ident[:], ones[:], ACT.Square, scale=0.0)
+        zero(w1cs)
         zero(w2s)
-        nc.vector.tensor_tensor_scan(column[:], ones[:], ones[:], 0.0, ALU.mult, ALU.add)
+        zero(w1hs)
+        nc.gpsimd.memset(xs_hot[:].bitcast(I32), 0)
+        load_scales(nc.scalar, w1hs, W1H_ROW, w1h_scales)
+        for q in range(4):
+            nc.scalar.dma_start(xs_hot[32 * q : 32 * q + 8, :].bitcast(I32), x_scales[:, 4 * q : 4 * q + 4, :].bitcast(I32))
+        nc.vector.tensor_tensor_scan(column[:], ones[:, 0:32], ones[:, 0:32], 0.0, ALU.mult, ALU.add)
         nc.vector.transpose(row[:], column[:])
         for q in range(4):
             part = slice(32 * q, 32 * q + 32)
             nc.vector.tensor_tensor(ident[part, part], column[part, :], row[part, :], ALU.is_equal)
 
-        load_x(0)
+        nc.sync.dma_start(w1c_head[0][:].bitcast(I32), w1c_words[1].rearrange("s p b -> p s b").bitcast(I32))
         for r in range(4):
             nc.sync.dma_start(xs_cold[r:P:32, :, :].bitcast(I32), x_scales[:, r:16:4, :].rearrange("s q t -> q s t").bitcast(I32))
-        load_x(1)
         nc.sync.dma_start(offs_t[:], offs)
-        load_w1c(0)
-        load_scales(w1cs, 0, w1c_scales)
-        load_w1c(1)
-        load_w1c(2)
-        for q in range(4):
-            nc.sync.dma_start(xs_hot[32 * q : 32 * q + 8, :].bitcast(I32), x_scales[:, 4 * q : 4 * q + 4, :].bitcast(I32))
-        load_w1c(3)
-        load_w1c(4)
-        load_w1h(0)
-        load_scales(w1hs, W1H_ROW, w1h_scales)
-        for e in range(1, HOT):
+        nc.sync.dma_start(xw[:], x_words.rearrange("s p t d -> p s (t d)").bitcast(I32))
+        load_scales(nc.sync, w1cs, 0, w1c_scales)
+        nc.sync.dma_start(w1c_head[1][:].bitcast(I32), w1c_words[2].rearrange("s p b -> p s b").bitcast(I32))
+        nc.sync.dma_start(w1c_next[:].bitcast(I32), w1c_words[3:5].rearrange("e s p b -> p (e s) b").bitcast(I32))
+        nc.sync.dma_start(w1c_last[:].bitcast(I32), w1c_words[0].rearrange("s p b -> p s b").bitcast(I32))
+        for e in (4, 2, 3, 0, 1):
             load_w1h(e)
         nc.sync.dma_start(w2c[:].bitcast(I32), w2c_words.rearrange("e s p b -> p (e s) b").bitcast(I32))
-        load_scales(w2s[:, HOT:E, :], 0, w2c_scales)
+        load_scales(nc.sync, w2s[:, HOT:E, :], 0, w2c_scales)
         nc.sync.dma_start(w2h[:], w2h_words.rearrange("e s p n d -> p (e s) (n d)").bitcast(I32))
-        load_scales(w2s[:, 0:HOT, :], W2H_ROW, w2h_scales)
+        load_scales(nc.sync, w2s[:, 0:HOT, :], W2H_ROW, w2h_scales)
         nc.sync.dma_start(gates[:], gate.rearrange("r p t -> p r t"))
         nc.sync.dma_start(pos_t[0][:], pos1)
         nc.sync.dma_start(pos_t[1][:], pos2)
@@ -129,51 +121,63 @@ def tile_moe_hot_mlp_relu2_kernel(
         def listed(first, last):
             return offs_t[:, first * C // 16 : last * C // 16]
 
-        def gather_bytes(first, last):
-            if first < HOT:
-                nc.vector.tensor_copy(gs_hot[:, first * C : last * C], xs_hot[:].indirect(listed(first, last)))
-            else:
-                for s in range(PASSES):
-                    nc.vector.tensor_copy(
-                        gs_cold[s][:, (first - HOT) * C : (last - HOT) * C], xs_cold[:, s, :].indirect(listed(first, last))
-                    )
+        words = {}
+        scale_rows = {}
 
-        def gather_words(first, last):
+        def gather_words(first, tag):
+            tile = after(tag, f"words{first}", [P, PASSES, 2 * C], U32)
             for s in range(PASSES):
-                nc.vector.tensor_copy(gw[s][:, first * C : last * C], xw[s][:].bitcast(U32).indirect(listed(first, last)))
+                nc.vector.tensor_copy(tile[:, s, :], xw[:, s, :].bitcast(U32).indirect(listed(first, first + 2)))
+                for u in range(2):
+                    words[first + u, s] = tile[:, s, u * C : (u + 1) * C]
 
-        for first, last in ((5, 8), (8, 10)):
-            gather_bytes(first, last)
-            gather_words(first, last)
-        for first, last in ((0, 2), (2, 5)):
-            gather_bytes(first, last)
-            for e in range(first, last):
-                gather_words(e, e + 1)
+        def gather_cold_bytes(first, tag):
+            tile = after(tag, f"bytes{first}", [P, PASSES, 2 * C], U8)
+            for s in range(PASSES):
+                nc.vector.tensor_copy(tile[:, s, :], xs_cold[:, s, :].indirect(listed(first, first + 2)))
+                for u in range(2):
+                    scale_rows[first + u, s] = tile[:, s, u * C : (u + 1) * C]
+
+        def gather_hot_bytes(first, tag):
+            mixed = first + 1 == HOT
+            tile = after(tag, f"bytes{first}", [P, (3 if mixed else 2) * C], U8)
+            nc.vector.tensor_copy(tile[:, 0 : 2 * C], xs_hot[:].indirect(listed(first, first + 2)))
+            for u in range(2):
+                for s in range(PASSES):
+                    scale_rows[first + u, s] = tile[4 * s : P, u * C : (u + 1) * C]
+            if mixed:
+                nc.vector.tensor_copy(tile[:, 2 * C : 3 * C], xs_cold[:, 1, :].indirect(listed(HOT, HOT + 1)))
+                scale_rows[HOT, 1] = tile[:, 2 * C : 3 * C]
 
         relus = {}
 
-        def first_layer(j):
+        def first_pass(j, s):
             e = ORDER[j]
-            cols = slice(e * C, (e + 1) * C)
-            for s in range(PASSES):
-                if e < HOT:
-                    x_scale = gs_hot[4 * s : P, cols]
-                    w = w1h[e][:, s, :].bitcast(FP8X4)
-                    w_scale = w1hs[W1H_ROW:P, e * PASSES + s, :]
+            if e < HOT:
+                w = w1h[e][:, s, :].bitcast(FP8X4)
+                w_scale = w1hs[W1H_ROW:P, e * PASSES + s, :]
+            else:
+                f = e - HOT
+                if f == 0:
+                    w = w1c_last[:, s, :].bitcast(FP4X4)
+                elif f < 3:
+                    w = w1c_head[f - 1][:, s, :].bitcast(FP4X4)
                 else:
-                    f = e - HOT
-                    x_scale = gs_cold[s][:, f * C : (f + 1) * C]
-                    w = w1c[f][:, s, :].bitcast(FP4X4)
-                    w_scale = w1cs[:, f * PASSES + s, :]
-                nc.tensor.matmul_mx(
-                    out=v_banks[j % 3][:], lhsT=gw[s][:, cols].bitcast(FP8X4), lhsT_scale=x_scale,
-                    rhs=w, rhs_scale=w_scale, start=(s == 0), stop=(s == PASSES - 1),
-                )
+                    w = w1c_next[:, (f - 3) * PASSES + s, :].bitcast(FP4X4)
+                w_scale = w1cs[:, f * PASSES + s, :]
+            nc.tensor.matmul_mx(
+                out=v_bank[j][:], lhsT=words[e, s].bitcast(FP8X4), lhsT_scale=scale_rows[e, s],
+                rhs=w, rhs_scale=w_scale, start=(s == 0), stop=(s == PASSES - 1),
+            )
+
+        def first_layer(j):
+            for s in range(PASSES):
+                first_pass(j, s)
 
         def relu(j):
             r = ring.tile([P, 4, P], F32, name="r", align_bytes=64)
             relus[j] = r
-            v_by_t = v_banks[j % 3][:].rearrange("j (p t) -> j t p", t=4)
+            v_by_t = v_bank[j][:].rearrange("j (p t) -> j t p", t=4)
             if j in VECTOR_RELU:
                 nc.vector.tensor_scalar(r[:], v_by_t, 0.0, None, ALU.max)
             else:
@@ -181,10 +185,11 @@ def tile_moe_hot_mlp_relu2_kernel(
 
         def turn(j):
             for t in range(4):
-                nc.tensor.transpose(t_banks[j % 2][:, t, :], relus[j][:, t, :], ident[:])
+                nc.tensor.transpose(t_bank[j][:, t * C : (t + 1) * C], relus[j][:, t, :], ident[:])
 
         def square(j):
-            nc.scalar.activation(h_all[:, j * C : (j + 1) * C, :], t_banks[j % 2][:].rearrange("p t j -> p j t"), ACT.Square)
+            e = ORDER[j]
+            nc.scalar.activation(h_all[:, e * C : (e + 1) * C, :], t_bank[j][:].rearrange("p (t j) -> p j t", t=4), ACT.Square)
 
         def quantise(first, last):
             cols = slice(first * C, last * C)
@@ -193,42 +198,63 @@ def tile_moe_hot_mlp_relu2_kernel(
                 in_=h_all[:, cols, :].rearrange("p j t -> p (j t)"),
             )
 
-        def second_layer(j, bank, place):
-            e = ORDER[j]
-            cols = slice(j * C, (j + 1) * C)
-            if e < HOT:
-                w = w2h[:, e, :].bitcast(FP8X4)
-                w_scale = w2s[W2H_ROW:P, e, :]
-            else:
-                w = w2c[:, e - HOT, :].bitcast(FP4X4)
-                w_scale = w2s[:, e, :]
-            nc.tensor.matmul_mx(
-                out=bank[:, place * C : (place + 1) * C], lhsT=w, lhsT_scale=w_scale,
-                rhs=h_words[:, cols].bitcast(FP8X4), rhs_scale=h_scale[:, cols], start=True, stop=True,
-            )
+        def second_layer(first, last, bank):
+            for e in range(first, last):
+                cols = slice(e * C, (e + 1) * C)
+                if e < HOT:
+                    w = w2h[:, e, :].bitcast(FP8X4)
+                    w_scale = w2s[W2H_ROW:P, e, :]
+                else:
+                    w = w2c[:, e - HOT, :].bitcast(FP4X4)
+                    w_scale = w2s[:, e, :]
+                nc.tensor.matmul_mx(
+                    out=bank[:, (e - first) * C : (e - first + 1) * C], lhsT=w, lhsT_scale=w_scale,
+                    rhs=h_words[:, cols].bitcast(FP8X4), rhs_scale=h_scale[:, cols], start=True, stop=True,
+                )
 
+        gather_cold_bytes(6, "bytes_a")
+        gather_words(6, "words_a")
+        gather_words(8, "words_b")
         first_layer(0)
         first_layer(1)
+        gather_cold_bytes(8, "head0")
+        gather_words(4, "words_a")
+        gather_hot_bytes(4, "bytes_a")
         relu(0)
-        for j in range(E):
+        relu(1)
+        turn(0)
+        for j in (2, 4, 6, 8):
+            square(j - 2)
+            first_layer(j)
+            first_layer(j + 1)
+            if j == 2:
+                gather_words(2, "words_b")
+                gather_hot_bytes(2, "head0")
+                gather_words(0, "next")
+            if j == 4:
+                gather_hot_bytes(0, "bytes_a")
+            if j == 8:
+                quantise(6, 10)
+                second_layer(6, 10, banks[5])
+            relu(j)
+            relu(j + 1)
+            turn(j - 1)
+            square(j - 1)
             turn(j)
-            if j + 2 < E:
-                first_layer(j + 2)
-            if j + 1 < E:
-                relu(j + 1)
-            square(j)
-        for first, last in ((0, 4), (4, 8), (8, 9), (9, 10)):
-            quantise(first, last)
-        for j in range(4):
-            second_layer(j, v_banks[2], j)
-        nc.vector.tensor_copy(y_all[:, 5 * C : 9 * C], v_banks[2][:])
-        for j in range(4, 8):
-            second_layer(j, v_banks[0], j - 4)
-        nc.scalar.copy(y_all[:, 9 * C : 10 * C], v_banks[0][:, 0:C])
-        nc.scalar.copy(y_all[:, 0 : 3 * C], v_banks[0][:, C : 4 * C])
-        for j in range(8, 10):
-            second_layer(j, last_bank, j - 8)
-        nc.scalar.copy(y_all[:, 3 * C : 5 * C], last_bank[:])
+        turn(9)
+        square(8)
+        square(9)
+        quantise(4, 6)
+        second_layer(4, 6, banks[6])
+        nc.vector.tensor_copy(y_all[:, 6 * C : 10 * C], banks[5][:])
+        quantise(2, 4)
+        nc.vector.tensor_copy(y_all[:, 4 * C : 6 * C], banks[6][:, 0 : 2 * C])
+        second_layer(2, 4, banks[7])
+        quantise(0, 1)
+        nc.vector.tensor_copy(y_all[:, 2 * C : 4 * C], banks[7][:, 0 : 2 * C])
+        quantise(1, 2)
+        second_layer(0, 2, banks[0])
+        nc.scalar.copy(y_all[:, 0 : 2 * C], banks[0][:, 0 : 2 * C])
 
         HALF = T // 2
         parts = [[kept(f"part{r}{u}", [P, HALF], F32) for r in range(2)] for u in range(2)]

@@ -48,7 +48,8 @@ def tile_moe_hot_mlp_relu2_kernel(
         xs_cold_tile = kept("xs_cold", [P, PASSES * T + 4], U8)
         xs_cold = xs_cold_tile[:, 0 : PASSES * T].rearrange("p (s t) -> p s t", s=PASSES)
         xs_hot = kept("xs_hot", [P, T], U8)
-        w1h = [kept(f"w1h{e}", [P, PASSES, H], I32) for e in range(HOT)]
+        w1h = {e: kept(f"w1h{e}", [P, PASSES, H], I32) for e in range(HOT) if e != ORDER[-1]}
+        w1h_last = [kept(f"w1h_last{s}", [P, H], I32) for s in range(PASSES)]
         w1c_head = [after(f"head{u}", f"w1c_head{u}", [P, PASSES, 2 * H], U8) for u in range(2)]
         w1c_next = after("next", "w1c_next", [P, 2 * PASSES, 2 * H], U8)
         w1c_last = kept("w1c_last", [P, PASSES, 2 * H], U8)
@@ -81,7 +82,11 @@ def tile_moe_hot_mlp_relu2_kernel(
                 )
 
         def load_w1h(e):
-            nc.sync.dma_start(w1h[e][:], w1h_words[e].rearrange("s p i d -> p s (i d)").bitcast(I32))
+            if e == ORDER[-1]:
+                for s in range(PASSES):
+                    nc.sync.dma_start(w1h_last[s][:], w1h_words[e, s].rearrange("p i d -> p (i d)").bitcast(I32))
+            else:
+                nc.sync.dma_start(w1h[e][:], w1h_words[e].rearrange("s p i d -> p s (i d)").bitcast(I32))
 
         nc.vector.memset(xs_cold_tile[:, 0 : PASSES * T + 4].bitcast(I32), 0)
         nc.gpsimd.memset(ones[:], 1.0)
@@ -154,7 +159,7 @@ def tile_moe_hot_mlp_relu2_kernel(
         def first_pass(j, s):
             e = ORDER[j]
             if e < HOT:
-                w = w1h[e][:, s, :].bitcast(FP8X4)
+                w = (w1h_last[s][:] if e == ORDER[-1] else w1h[e][:, s, :]).bitcast(FP8X4)
                 w_scale = w1hs[W1H_ROW:P, e * PASSES + s, :]
             else:
                 f = e - HOT
@@ -178,7 +183,10 @@ def tile_moe_hot_mlp_relu2_kernel(
             r = ring.tile([P, 4, P], F32, name="r", align_bytes=64)
             relus[j] = r
             v_by_t = v_bank[j][:].rearrange("j (p t) -> j t p", t=4)
-            if j in VECTOR_RELU:
+            if j == E - 1:
+                for t in (0, 2):
+                    nc.vector.tensor_scalar(r[:, t : t + 2, :], v_by_t[:, t : t + 2, :], 0.0, None, ALU.max)
+            elif j in VECTOR_RELU:
                 nc.vector.tensor_scalar(r[:], v_by_t, 0.0, None, ALU.max)
             else:
                 nc.scalar.activation(r[:], v_by_t, ACT.Relu)
@@ -246,15 +254,17 @@ def tile_moe_hot_mlp_relu2_kernel(
         square(9)
         quantise(4, 6)
         second_layer(4, 6, banks[6])
-        nc.vector.tensor_copy(y_all[:, 6 * C : 10 * C], banks[5][:])
+        nc.scalar.copy(y_all[:, 6 * C : 10 * C], banks[5][:])
         quantise(2, 4)
         nc.vector.tensor_copy(y_all[:, 4 * C : 6 * C], banks[6][:, 0 : 2 * C])
         second_layer(2, 4, banks[7])
         quantise(0, 1)
         nc.vector.tensor_copy(y_all[:, 2 * C : 4 * C], banks[7][:, 0 : 2 * C])
         quantise(1, 2)
-        second_layer(0, 2, banks[0])
-        nc.scalar.copy(y_all[:, 0 : 2 * C], banks[0][:, 0 : 2 * C])
+        second_layer(0, 1, banks[0])
+        nc.scalar.copy(y_all[:, 0:C], banks[0][:, 0:C])
+        second_layer(1, 2, banks[1])
+        nc.vector.tensor_copy(y_all[:, C : 2 * C], banks[1][:, 0:C])
 
         HALF = T // 2
         parts = [[kept(f"part{r}{u}", [P, HALF], F32) for r in range(2)] for u in range(2)]

@@ -58,7 +58,7 @@ def tile_moe_hot_mlp_relu2_kernel(
         w1hs = kept("w1hs", [P, HOT * PASSES, H], U8)
         w1cs = kept("w1cs", [P, COLD * PASSES, H], U8)
         w2s = kept("w2s", [P, E, N], U8)
-        gates = kept("gates", [P, 2, T], F32)
+        gates = [kept(f"gate{r}", [P, T], F32) for r in range(2)]
         y_all = kept("y_all", [P, SLOTS], F32)
         ident = kept("ident", [P, P], F32)
         h_all = kept("h_all", [P, SLOTS, 4], BF16)
@@ -115,13 +115,14 @@ def tile_moe_hot_mlp_relu2_kernel(
         nc.sync.dma_start(w1c_last[:].bitcast(I32), w1c_words[0].rearrange("s p b -> p s b").bitcast(I32))
         for e in (4, 2, 3, 0, 1):
             load_w1h(e)
-        nc.sync.dma_start(w2c[:].bitcast(I32), w2c_words.rearrange("e s p b -> p (e s) b").bitcast(I32))
         load_scales(nc.sync, w2s[:, HOT:E, :], 0, w2c_scales)
+        nc.sync.dma_start(w2c[:].bitcast(I32), w2c_words.rearrange("e s p b -> p (e s) b").bitcast(I32))
         nc.sync.dma_start(w2h[:], w2h_words.rearrange("e s p n d -> p (e s) (n d)").bitcast(I32))
         load_scales(nc.sync, w2s[:, 0:HOT, :], W2H_ROW, w2h_scales)
-        nc.sync.dma_start(gates[:], gate.rearrange("r p t -> p r t"))
         nc.sync.dma_start(pos_t[0][:], pos1)
         nc.sync.dma_start(pos_t[1][:], pos2)
+        for r in range(2):
+            nc.sync.dma_start(gates[r][:], gate[r])
 
         def listed(first, last):
             return offs_t[:, first * C // 16 : last * C // 16]
@@ -272,15 +273,15 @@ def tile_moe_hot_mlp_relu2_kernel(
 
         def fetch(u, r):
             a, b = u * HALF, (u + 1) * HALF
-            nc.vector.tensor_tensor(parts[u][r][:], y_all[:].indirect(pos_t[r][:, a // 16 : b // 16]), gates[:, r, a:b], ALU.mult)
+            nc.vector.tensor_tensor(parts[u][r][:], y_all[:].indirect(pos_t[r][:, a // 16 : b // 16]), gates[r][:, a:b], ALU.mult)
 
         def finish(u):
             nc.vector.tensor_tensor(total[u][:], parts[u][0][:], parts[u][1][:], ALU.add)
             nc.sync.dma_start(out[:, u * HALF : (u + 1) * HALF], total[u][:])
 
         fetch(0, 0)
-        fetch(0, 1)
         fetch(1, 0)
-        finish(0)
+        fetch(0, 1)
         fetch(1, 1)
+        finish(0)
         finish(1)

@@ -45,8 +45,7 @@ def tile_moe_hot_mlp_relu2_kernel(
         offs_t = keep.tile([P, SLOTS // 16], U16, name="offs_t")
         pos_t = [keep.tile([P, T // 16], U16, name=f"pos_t{r}") for r in range(2)]
         xw = kept("xw", [P, PASSES, T], I32)
-        xs_cold_tile = kept("xs_cold", [P, PASSES * T + 4], U8)
-        xs_cold = xs_cold_tile[:, 0 : PASSES * T].rearrange("p (s t) -> p s t", s=PASSES)
+        xs_cold = kept("xs_cold", [P, PASSES, T], U8)
         xs_hot = kept("xs_hot", [P, T], U8)
         w1h = {e: kept(f"w1h{e}", [P, PASSES, H], I32) for e in range(HOT) if e != ORDER[-1]}
         w1h_last = [kept(f"w1h_last{s}", [P, H], I32) for s in range(PASSES)]
@@ -71,8 +70,8 @@ def tile_moe_hot_mlp_relu2_kernel(
         v_bank = [banks[j % 2] for j in range(E)]
         t_bank = [banks[i] for i in (2, 3, 2, 3, 2, 5, 2, 3, 2, 4)]
 
-        def zero(plane):
-            nc.gpsimd.memset(plane[:].rearrange("p a b -> p (a b)").bitcast(I32), 0)
+        def zero(engine, plane):
+            engine.memset(plane[:].rearrange("p a b -> p (a b)").bitcast(I32), 0)
 
         def load_scales(queue, plane, first, scales):
             for r in range(4):
@@ -88,18 +87,19 @@ def tile_moe_hot_mlp_relu2_kernel(
             else:
                 nc.sync.dma_start(w1h[e][:], w1h_words[e].rearrange("s p i d -> p s (i d)").bitcast(I32))
 
-        nc.vector.memset(xs_cold_tile[:, 0 : PASSES * T + 4].bitcast(I32), 0)
-        nc.gpsimd.memset(ones[:], 1.0)
+        zero(nc.gpsimd, xs_cold)
+        zero(nc.vector, w2s)
+        load_scales(nc.gpsimd, w2s[:, 0:HOT, :], W2H_ROW, w2h_scales)
+        nc.vector.memset(ones[:], 1.0)
         nc.scalar.activation(ident[:], ones[:], ACT.Square, scale=0.0)
-        zero(w1cs)
-        zero(w2s)
-        zero(w1hs)
-        nc.gpsimd.memset(xs_hot[:].bitcast(I32), 0)
+        zero(nc.vector, w1cs)
+        nc.vector.tensor_tensor_scan(column[:], ones[:, 0:32], ones[:, 0:32], 0.0, ALU.mult, ALU.add)
+        nc.vector.transpose(row[:], column[:])
+        zero(nc.vector, w1hs)
+        nc.vector.memset(xs_hot[:].bitcast(I32), 0)
         load_scales(nc.scalar, w1hs, W1H_ROW, w1h_scales)
         for q in range(4):
             nc.scalar.dma_start(xs_hot[32 * q : 32 * q + 8, :].bitcast(I32), x_scales[:, 4 * q : 4 * q + 4, :].bitcast(I32))
-        nc.vector.tensor_tensor_scan(column[:], ones[:, 0:32], ones[:, 0:32], 0.0, ALU.mult, ALU.add)
-        nc.vector.transpose(row[:], column[:])
         for q in range(4):
             part = slice(32 * q, 32 * q + 32)
             nc.vector.tensor_tensor(ident[part, part], column[part, :], row[part, :], ALU.is_equal)
@@ -118,7 +118,6 @@ def tile_moe_hot_mlp_relu2_kernel(
         load_scales(nc.sync, w2s[:, HOT:E, :], 0, w2c_scales)
         nc.sync.dma_start(w2c[:].bitcast(I32), w2c_words.rearrange("e s p b -> p (e s) b").bitcast(I32))
         nc.sync.dma_start(w2h[:], w2h_words.rearrange("e s p n d -> p (e s) (n d)").bitcast(I32))
-        load_scales(nc.sync, w2s[:, 0:HOT, :], W2H_ROW, w2h_scales)
         nc.sync.dma_start(pos_t[0][:], pos1)
         nc.sync.dma_start(pos_t[1][:], pos2)
         for r in range(2):
@@ -260,7 +259,7 @@ def tile_moe_hot_mlp_relu2_kernel(
         nc.vector.tensor_copy(y_all[:, 4 * C : 6 * C], banks[6][:, 0 : 2 * C])
         second_layer(2, 4, banks[7])
         quantise(0, 1)
-        nc.vector.tensor_copy(y_all[:, 2 * C : 4 * C], banks[7][:, 0 : 2 * C])
+        nc.scalar.copy(y_all[:, 2 * C : 4 * C], banks[7][:, 0 : 2 * C])
         quantise(1, 2)
         second_layer(0, 1, banks[0])
         nc.scalar.copy(y_all[:, 0:C], banks[0][:, 0:C])

@@ -118,10 +118,9 @@ def tile_moe_hot_mlp_relu2_kernel(
         load_scales(nc.sync, w2s[:, HOT:E, :], 0, w2c_scales)
         nc.sync.dma_start(w2c[:].bitcast(I32), w2c_words.rearrange("e s p b -> p (e s) b").bitcast(I32))
         nc.sync.dma_start(w2h[:], w2h_words.rearrange("e s p n d -> p (e s) (n d)").bitcast(I32))
-        nc.sync.dma_start(pos_t[0][:], pos1)
-        nc.sync.dma_start(pos_t[1][:], pos2)
-        for r in range(2):
+        for r, pos in enumerate((pos1, pos2)):
             nc.sync.dma_start(gates[r][:], gate[r])
+            nc.sync.dma_start(pos_t[r][:], pos)
 
         def listed(first, last):
             return offs_t[:, first * C // 16 : last * C // 16]

@@ -24,6 +24,7 @@ ORDER = (6, 7, 8, 9, 5, 4, 2, 3, 0, 1)
 W1H_ROW = 12
 W2H_ROW = 8
 VECTOR_RELU = (7, 8, 9)
+CUTS = (0, 256, 448, 640)
 
 
 def tile_moe_hot_mlp_relu2_kernel(
@@ -57,7 +58,7 @@ def tile_moe_hot_mlp_relu2_kernel(
         w1hs = kept("w1hs", [P, HOT * PASSES, H], U8)
         w1cs = kept("w1cs", [P, COLD * PASSES, H], U8)
         w2s = kept("w2s", [P, E, N], U8)
-        gates = [kept(f"gate{r}", [P, T], F32) for r in range(2)]
+        gates = kept("gates", [P, 2, T], F32)
         y_all = kept("y_all", [P, SLOTS], F32)
         ident = kept("ident", [P, P], F32)
         h_all = kept("h_all", [P, SLOTS, 4], BF16)
@@ -119,7 +120,7 @@ def tile_moe_hot_mlp_relu2_kernel(
         nc.sync.dma_start(w2c[:].bitcast(I32), w2c_words.rearrange("e s p b -> p (e s) b").bitcast(I32))
         nc.sync.dma_start(w2h[:], w2h_words.rearrange("e s p n d -> p (e s) (n d)").bitcast(I32))
         for r, pos in enumerate((pos1, pos2)):
-            nc.sync.dma_start(gates[r][:], gate[r])
+            nc.sync.dma_start(gates[:, r, :], gate[r])
             nc.sync.dma_start(pos_t[r][:], pos)
 
         def listed(first, last):
@@ -265,21 +266,31 @@ def tile_moe_hot_mlp_relu2_kernel(
         second_layer(1, 2, banks[1])
         nc.vector.tensor_copy(y_all[:, C : 2 * C], banks[1][:, 0:C])
 
-        HALF = T // 2
-        parts = [[kept(f"part{r}{u}", [P, HALF], F32) for r in range(2)] for u in range(2)]
-        total = [kept(f"total{u}", [P, HALF], F32) for u in range(2)]
+        pieces = list(zip(CUTS, CUTS[1:]))
+        fetched = {u: kept(f"fetched{u}", [P, 2, b - a], F32) for u, (a, b) in enumerate(pieces) if u > 0}
+        parts = [kept(f"parts{u}", [P, 2, b - a], F32) for u, (a, b) in enumerate(pieces)]
+        total = [kept(f"total{u}", [P, b - a], F32) for u, (a, b) in enumerate(pieces)]
 
-        def fetch(u, r):
-            a, b = u * HALF, (u + 1) * HALF
-            nc.vector.tensor_tensor(parts[u][r][:], y_all[:].indirect(pos_t[r][:, a // 16 : b // 16]), gates[r][:, a:b], ALU.mult)
+        def picked(u, r):
+            a, b = pieces[u]
+            return y_all[:].indirect(pos_t[r][:, a // 16 : b // 16])
 
         def finish(u):
-            nc.vector.tensor_tensor(total[u][:], parts[u][0][:], parts[u][1][:], ALU.add)
-            nc.sync.dma_start(out[:, u * HALF : (u + 1) * HALF], total[u][:])
+            a, b = pieces[u]
+            nc.vector.tensor_tensor(total[u][:], parts[u][:, 0, :], parts[u][:, 1, :], ALU.add)
+            nc.sync.dma_start(out[:, a:b], total[u][:])
 
-        fetch(0, 0)
-        fetch(1, 0)
-        fetch(0, 1)
-        fetch(1, 1)
+        def weigh(u):
+            a, b = pieces[u]
+            nc.vector.tensor_tensor(parts[u][:], fetched[u][:], gates[:, :, a:b], ALU.mult)
+
+        for r in range(2):
+            nc.vector.tensor_tensor(parts[0][:, r, :], picked(0, r), gates[:, r, CUTS[0] : CUTS[1]], ALU.mult)
+        for u in (1, 2):
+            for r in range(2):
+                nc.scalar.activation(fetched[u][:, r, :], picked(u, r), ACT.Copy)
+        weigh(1)
         finish(0)
+        weigh(2)
         finish(1)
+        finish(2)

@@ -34,7 +34,7 @@ def tile_moe_hot_mlp_relu2_kernel(
     nc = tc.nc
     with ExitStack() as ctx:
         keep = ctx.enter_context(tc.tile_pool(name="keep", bufs=1))
-        ring = ctx.enter_context(tc.tile_pool(name="ring", bufs=4))
+        ring = ctx.enter_context(tc.tile_pool(name="ring", bufs=6))
         psum = ctx.enter_context(tc.psum_pool(name="psum", bufs=1))
 
         def kept(name, shape, dtype):
@@ -68,8 +68,8 @@ def tile_moe_hot_mlp_relu2_kernel(
         column = kept("column", [P, 32], F32)
         row = kept("row", [P, 32], F32)
         banks = [psum.tile([P, H], F32, name=f"bank{i}") for i in range(8)]
-        v_bank = [banks[j % 2] for j in range(E)]
-        t_bank = [banks[i] for i in (2, 3, 2, 3, 2, 5, 2, 3, 2, 4)]
+        v_bank = [banks[j % 6] for j in range(E)]
+        t_bank = [banks[(j ^ 1) % 6] if j < E - 2 else banks[j % 6] for j in range(E)]
 
         def zero(engine, plane):
             engine.memset(plane[:].rearrange("p a b -> p (a b)").bitcast(I32), 0)
@@ -129,11 +129,11 @@ def tile_moe_hot_mlp_relu2_kernel(
         words = {}
         scale_rows = {}
 
-        def gather_words(first, tag):
-            tile = after(tag, f"words{first}", [P, PASSES, 2 * C], U32)
+        def gather_words(first, tag, count=2):
+            tile = after(tag, f"words{first}", [P, PASSES, count * C], U32)
             for s in range(PASSES):
-                nc.vector.tensor_copy(tile[:, s, :], xw[:, s, :].bitcast(U32).indirect(listed(first, first + 2)))
-                for u in range(2):
+                nc.vector.tensor_copy(tile[:, s, :], xw[:, s, :].bitcast(U32).indirect(listed(first, first + count)))
+                for u in range(count):
                     words[first + u, s] = tile[:, s, u * C : (u + 1) * C]
 
         def gather_cold_bytes(first, tag):
@@ -144,15 +144,11 @@ def tile_moe_hot_mlp_relu2_kernel(
                     scale_rows[first + u, s] = tile[:, s, u * C : (u + 1) * C]
 
         def gather_hot_bytes(first, tag):
-            mixed = first + 1 == HOT
-            tile = after(tag, f"bytes{first}", [P, (3 if mixed else 2) * C], U8)
+            tile = after(tag, f"bytes{first}", [P, 2 * C], U8)
             nc.vector.tensor_copy(tile[:, 0 : 2 * C], xs_hot[:].indirect(listed(first, first + 2)))
             for u in range(2):
                 for s in range(PASSES):
                     scale_rows[first + u, s] = tile[4 * s : P, u * C : (u + 1) * C]
-            if mixed:
-                nc.vector.tensor_copy(tile[:, 2 * C : 3 * C], xs_cold[:, 1, :].indirect(listed(HOT, HOT + 1)))
-                scale_rows[HOT, 1] = tile[:, 2 * C : 3 * C]
 
         relus = {}
 
@@ -221,50 +217,53 @@ def tile_moe_hot_mlp_relu2_kernel(
                 )
 
         gather_cold_bytes(6, "bytes_a")
-        gather_words(6, "words_a")
+        gather_cold_bytes(8, "bytes_b")
+        fifth = kept("bytes_fifth", [P, C], U8)
+        nc.vector.tensor_copy(fifth[:], xs_cold[:, 1, :].indirect(listed(HOT, HOT + 1)))
+        gather_words(6, "words_first", 1)
+        gather_words(7, "words_a", 1)
         gather_words(8, "words_b")
+        gather_words(4, "words_c")
+        gather_hot_bytes(4, "bytes_c")
+        scale_rows[HOT, 1] = fifth[:]
+        gather_hot_bytes(2, "bytes_d")
+        gather_hot_bytes(0, "bytes_e")
         first_layer(0)
         first_layer(1)
-        gather_cold_bytes(8, "head0")
-        gather_words(4, "words_a")
-        gather_hot_bytes(4, "bytes_a")
+        gather_words(2, "words_a")
         relu(0)
         relu(1)
-        turn(0)
         for j in (2, 4, 6, 8):
-            square(j - 2)
             first_layer(j)
             first_layer(j + 1)
             if j == 2:
-                gather_words(2, "words_b")
-                gather_hot_bytes(2, "head0")
-                gather_words(0, "next")
-            if j == 4:
-                gather_hot_bytes(0, "bytes_a")
+                gather_words(0, "words_b")
             if j == 8:
                 quantise(6, 10)
-                second_layer(6, 10, banks[5])
             relu(j)
             relu(j + 1)
+            turn(j - 2)
             turn(j - 1)
+            square(j - 2)
             square(j - 1)
-            turn(j)
+        turn(8)
         turn(9)
         square(8)
         square(9)
+        second_layer(6, 10, banks[6])
         quantise(4, 6)
-        second_layer(4, 6, banks[6])
-        nc.scalar.copy(y_all[:, 6 * C : 10 * C], banks[5][:])
+        second_layer(4, 6, banks[7])
+        nc.scalar.copy(y_all[:, 6 * C : 10 * C], banks[6][:])
         quantise(2, 4)
-        nc.vector.tensor_copy(y_all[:, 4 * C : 6 * C], banks[6][:, 0 : 2 * C])
-        second_layer(2, 4, banks[7])
+        nc.vector.tensor_copy(y_all[:, 4 * C : 6 * C], banks[7][:, 0 : 2 * C])
+        second_layer(2, 4, banks[4])
         quantise(0, 1)
-        nc.scalar.copy(y_all[:, 2 * C : 4 * C], banks[7][:, 0 : 2 * C])
+        nc.scalar.copy(y_all[:, 2 * C : 4 * C], banks[4][:, 0 : 2 * C])
         quantise(1, 2)
-        second_layer(0, 1, banks[0])
-        nc.scalar.copy(y_all[:, 0:C], banks[0][:, 0:C])
-        second_layer(1, 2, banks[1])
-        nc.vector.tensor_copy(y_all[:, C : 2 * C], banks[1][:, 0:C])
+        second_layer(0, 1, banks[5])
+        nc.scalar.copy(y_all[:, 0:C], banks[5][:, 0:C])
+        second_layer(1, 2, banks[0])
+        nc.vector.tensor_copy(y_all[:, C : 2 * C], banks[0][:, 0:C])
 
         pieces = list(zip(CUTS, CUTS[1:]))
         fetched = {u: kept(f"fetched{u}", [P, 2, b - a], F32) for u, (a, b) in enumerate(pieces) if u > 0}

@@ -24,7 +24,7 @@ ORDER = (6, 7, 8, 9, 5, 4, 2, 3, 0, 1)
 W1H_ROW = 12
 W2H_ROW = 8
 VECTOR_RELU = (7, 8, 9)
-CUTS = (0, 256, 448, 640)
+CUTS = (0, 320, 512, 640)
 
 
 def tile_moe_hot_mlp_relu2_kernel(
@@ -218,18 +218,17 @@ def tile_moe_hot_mlp_relu2_kernel(
 
         gather_cold_bytes(6, "bytes_a")
         gather_cold_bytes(8, "bytes_b")
-        fifth = kept("bytes_fifth", [P, C], U8)
-        nc.vector.tensor_copy(fifth[:], xs_cold[:, 1, :].indirect(listed(HOT, HOT + 1)))
         gather_words(6, "words_first", 1)
         gather_words(7, "words_a", 1)
         gather_words(8, "words_b")
         gather_words(4, "words_c")
         gather_hot_bytes(4, "bytes_c")
-        scale_rows[HOT, 1] = fifth[:]
-        gather_hot_bytes(2, "bytes_d")
-        gather_hot_bytes(0, "bytes_e")
         first_layer(0)
+        fifth = after("words_first", "bytes_fifth", [P, C], U8)
+        nc.vector.tensor_copy(fifth[:], xs_cold[:, 1, :].indirect(listed(HOT, HOT + 1)))
+        scale_rows[HOT, 1] = fifth[:]
         first_layer(1)
+        gather_hot_bytes(2, "bytes_a")
         gather_words(2, "words_a")
         relu(0)
         relu(1)
@@ -237,6 +236,7 @@ def tile_moe_hot_mlp_relu2_kernel(
             first_layer(j)
             first_layer(j + 1)
             if j == 2:
+                gather_hot_bytes(0, "bytes_b")
                 gather_words(0, "words_b")
             if j == 8:
                 quantise(6, 10)

from contextlib import ExitStack

import concourse.mybir as mybir

K, T, E, C, H, N, HOT = 1024, 640, 10, 128, 512, 128, 5
COLD = E - HOT
SLOTS = E * C
P = 128
PASSES = K // 512
FLOPS = 2 * SLOTS * (K * H + H * N)

F32 = mybir.dt.float32
BF16 = mybir.dt.bfloat16
I32 = mybir.dt.int32
U32 = mybir.dt.uint32
U16 = mybir.dt.uint16
U8 = mybir.dt.uint8
FP8X4 = mybir.dt.float8_e4m3fn_x4
FP4X4 = mybir.dt.float4_e2m1fn_x4
ACT = mybir.ActivationFunctionType
ALU = mybir.AluOpType

ORDER = (6, 7, 8, 9, 5, 4, 2, 3, 0, 1)
W1H_ROW = 12
W2H_ROW = 8
VECTOR_RELU = (7, 8, 9)
CUTS = (0, 320, 512, 640)


def tile_moe_hot_mlp_relu2_kernel(
    tc, x_words, x_scales, w1h_words, w1h_scales, w2h_words, w2h_scales,
    w1c_words, w1c_scales, w2c_words, w2c_scales, gate, offs, pos1, pos2, out,
):
    nc = tc.nc
    with ExitStack() as ctx:
        keep = ctx.enter_context(tc.tile_pool(name="keep", bufs=1))
        ring = ctx.enter_context(tc.tile_pool(name="ring", bufs=6))
        psum = ctx.enter_context(tc.psum_pool(name="psum", bufs=1))

        def kept(name, shape, dtype):
            return keep.tile(shape, dtype, name=name, align_bytes=64)

        def after(tag, name, shape, dtype):
            return keep.tile(shape, dtype, name=name, tag=tag, align_bytes=64)

        offs_t = keep.tile([P, SLOTS // 16], U16, name="offs_t")
        pos_t = [keep.tile([P, T // 16], U16, name=f"pos_t{r}") for r in range(2)]
        xw = kept("xw", [P, PASSES, T], I32)
        xs_cold = kept("xs_cold", [P, PASSES, T], U8)
        xs_hot = kept("xs_hot", [P, T], U8)
        w1h = {e: kept(f"w1h{e}", [P, PASSES, H], I32) for e in range(HOT) if e != ORDER[-1]}
        w1h_last = [kept(f"w1h_last{s}", [P, H], I32) for s in range(PASSES)]
        w1c_head = [after(f"head{u}", f"w1c_head{u}", [P, PASSES, 2 * H], U8) for u in range(2)]
        w1c_next = after("next", "w1c_next", [P, 2 * PASSES, 2 * H], U8)
        w1c_last = kept("w1c_last", [P, PASSES, 2 * H], U8)
        w2h = kept("w2h", [P, HOT, N], I32)
        w2c = kept("w2c", [P, COLD, 2 * N], U8)
        w1hs = kept("w1hs", [P, HOT * PASSES, H], U8)
        w1cs = kept("w1cs", [P, COLD * PASSES, H], U8)
        w2s = kept("w2s", [P, E, N], U8)
        gates = kept("gates", [P, 2, T], F32)
        y_all = kept("y_all", [P, SLOTS], F32)
        ident = kept("ident", [P, P], F32)
        h_all = kept("h_all", [P, SLOTS, 4], BF16)
        h_words = kept("h_words", [P, SLOTS], U32)
        h_scale = kept("h_scale", [P, SLOTS], U8)
        ones = kept("ones", [P, P], F32)
        column = kept("column", [P, 32], F32)
        row = kept("row", [P, 32], F32)
        banks = [psum.tile([P, H], F32, name=f"bank{i}") for i in range(8)]
        v_bank = [banks[j % 6] for j in range(E)]
        t_bank = [banks[(j ^ 1) % 6] if j < E - 2 else banks[j % 6] for j in range(E)]

        def zero(engine, plane):
            engine.memset(plane[:].rearrange("p a b -> p (a b)").bitcast(I32), 0)

        def load_scales(queue, plane, first, scales):
            for r in range(4):
                queue.dma_start(
                    plane[first + r : P : 32, :, :].bitcast(I32),
                    scales[:, :, r:16:4, :].rearrange("e s q i -> q (e s) i").bitcast(I32),
                )

        def load_w1h(e):
            if e == ORDER[-1]:
                for s in range(PASSES):
                    nc.sync.dma_start(w1h_last[s][:], w1h_words[e, s].rearrange("p i d -> p (i d)").bitcast(I32))
            else:
                nc.sync.dma_start(w1h[e][:], w1h_words[e].rearrange("s p i d -> p s (i d)").bitcast(I32))

        zero(nc.gpsimd, xs_cold)
        zero(nc.vector, w2s)
        load_scales(nc.gpsimd, w2s[:, 0:HOT, :], W2H_ROW, w2h_scales)
        nc.vector.memset(ones[:], 1.0)
        nc.scalar.activation(ident[:], ones[:], ACT.Square, scale=0.0)
        zero(nc.vector, w1cs)
        nc.vector.tensor_tensor_scan(column[:], ones[:, 0:32], ones[:, 0:32], 0.0, ALU.mult, ALU.add)
        nc.vector.transpose(row[:], column[:])
        zero(nc.vector, w1hs)
        nc.vector.memset(xs_hot[:].bitcast(I32), 0)
        load_scales(nc.scalar, w1hs, W1H_ROW, w1h_scales)
        for q in range(4):
            nc.scalar.dma_start(xs_hot[32 * q : 32 * q + 8, :].bitcast(I32), x_scales[:, 4 * q : 4 * q + 4, :].bitcast(I32))
        for q in range(4):
            part = slice(32 * q, 32 * q + 32)
            nc.vector.tensor_tensor(ident[part, part], column[part, :], row[part, :], ALU.is_equal)

        nc.sync.dma_start(w1c_head[0][:].bitcast(I32), w1c_words[1].rearrange("s p b -> p s b").bitcast(I32))
        for r in range(4):
            nc.sync.dma_start(xs_cold[r:P:32, :, :].bitcast(I32), x_scales[:, r:16:4, :].rearrange("s q t -> q s t").bitcast(I32))
        nc.sync.dma_start(offs_t[:], offs)
        nc.sync.dma_start(xw[:], x_words.rearrange("s p t d -> p s (t d)").bitcast(I32))
        load_scales(nc.sync, w1cs, 0, w1c_scales)
        nc.sync.dma_start(w1c_head[1][:].bitcast(I32), w1c_words[2].rearrange("s p b -> p s b").bitcast(I32))
        nc.sync.dma_start(w1c_next[:].bitcast(I32), w1c_words[3:5].rearrange("e s p b -> p (e s) b").bitcast(I32))
        nc.sync.dma_start(w1c_last[:].bitcast(I32), w1c_words[0].rearrange("s p b -> p s b").bitcast(I32))
        for e in (4, 2, 3, 0, 1):
            load_w1h(e)
        load_scales(nc.sync, w2s[:, HOT:E, :], 0, w2c_scales)
        nc.sync.dma_start(w2c[:].bitcast(I32), w2c_words.rearrange("e s p b -> p (e s) b").bitcast(I32))
        nc.sync.dma_start(w2h[:], w2h_words.rearrange("e s p n d -> p (e s) (n d)").bitcast(I32))
        for r, pos in enumerate((pos1, pos2)):
            nc.sync.dma_start(gates[:, r, :], gate[r])
            nc.sync.dma_start(pos_t[r][:], pos)

        def listed(first, last):
            return offs_t[:, first * C // 16 : last * C // 16]

        words = {}
        scale_rows = {}

        def gather_words(first, tag, count=2):
            tile = after(tag, f"words{first}", [P, PASSES, count * C], U32)
            for s in range(PASSES):
                nc.vector.tensor_copy(tile[:, s, :], xw[:, s, :].bitcast(U32).indirect(listed(first, first + count)))
                for u in range(count):
                    words[first + u, s] = tile[:, s, u * C : (u + 1) * C]

        def gather_cold_bytes(first, tag):
            tile = after(tag, f"bytes{first}", [P, PASSES, 2 * C], U8)
            for s in range(PASSES):
                nc.vector.tensor_copy(tile[:, s, :], xs_cold[:, s, :].indirect(listed(first, first + 2)))
                for u in range(2):
                    scale_rows[first + u, s] = tile[:, s, u * C : (u + 1) * C]

        def gather_hot_bytes(first, tag):
            tile = after(tag, f"bytes{first}", [P, 2 * C], U8)
            nc.vector.tensor_copy(tile[:, 0 : 2 * C], xs_hot[:].indirect(listed(first, first + 2)))
            for u in range(2):
                for s in range(PASSES):
                    scale_rows[first + u, s] = tile[4 * s : P, u * C : (u + 1) * C]

        relus = {}

        def first_pass(j, s):
            e = ORDER[j]
            if e < HOT:
                w = (w1h_last[s][:] if e == ORDER[-1] else w1h[e][:, s, :]).bitcast(FP8X4)
                w_scale = w1hs[W1H_ROW:P, e * PASSES + s, :]
            else:
                f = e - HOT
                if f == 0:
                    w = w1c_last[:, s, :].bitcast(FP4X4)
                elif f < 3:
                    w = w1c_head[f - 1][:, s, :].bitcast(FP4X4)
                else:
                    w = w1c_next[:, (f - 3) * PASSES + s, :].bitcast(FP4X4)
                w_scale = w1cs[:, f * PASSES + s, :]
            nc.tensor.matmul_mx(
                out=v_bank[j][:], lhsT=words[e, s].bitcast(FP8X4), lhsT_scale=scale_rows[e, s],
                rhs=w, rhs_scale=w_scale, start=(s == 0), stop=(s == PASSES - 1),
            )

        def first_layer(j):
            for s in range(PASSES):
                first_pass(j, s)

        def relu(j):
            r = ring.tile([P, 4, P], F32, name="r", align_bytes=64)
            relus[j] = r
            v_by_t = v_bank[j][:].rearrange("j (p t) -> j t p", t=4)
            if j == E - 1:
                for t in (0, 2):
                    nc.vector.tensor_scalar(r[:, t : t + 2, :], v_by_t[:, t : t + 2, :], 0.0, None, ALU.max)
            elif j in VECTOR_RELU:
                nc.vector.tensor_scalar(r[:], v_by_t, 0.0, None, ALU.max)
            else:
                nc.scalar.activation(r[:], v_by_t, ACT.Relu)

        def turn(j):
            for t in range(4):
                nc.tensor.transpose(t_bank[j][:, t * C : (t + 1) * C], relus[j][:, t, :], ident[:])

        def square(j):
            e = ORDER[j]
            nc.scalar.activation(h_all[:, e * C : (e + 1) * C, :], t_bank[j][:].rearrange("p (t j) -> p j t", t=4), ACT.Square)

        def quantise(first, last):
            cols = slice(first * C, last * C)
            nc.vector.quantize_mx(
                out=h_words[:, cols].bitcast(FP8X4), scales=h_scale[:, cols],
                in_=h_all[:, cols, :].rearrange("p j t -> p (j t)"),
            )

        def second_layer(first, last, bank):
            for e in range(first, last):
                cols = slice(e * C, (e + 1) * C)
                if e < HOT:
                    w = w2h[:, e, :].bitcast(FP8X4)
                    w_scale = w2s[W2H_ROW:P, e, :]
                else:
                    w = w2c[:, e - HOT, :].bitcast(FP4X4)
                    w_scale = w2s[:, e, :]
                nc.tensor.matmul_mx(
                    out=bank[:, (e - first) * C : (e - first + 1) * C], lhsT=w, lhsT_scale=w_scale,
                    rhs=h_words[:, cols].bitcast(FP8X4), rhs_scale=h_scale[:, cols], start=True, stop=True,
                )

        gather_cold_bytes(6, "bytes_a")
        gather_cold_bytes(8, "bytes_b")
        gather_words(6, "words_first", 1)
        gather_words(7, "words_a", 1)
        gather_words(8, "words_b")
        gather_words(4, "words_c")
        gather_hot_bytes(4, "bytes_c")
        first_layer(0)
        fifth = after("words_first", "bytes_fifth", [P, C], U8)
        nc.vector.tensor_copy(fifth[:], xs_cold[:, 1, :].indirect(listed(HOT, HOT + 1)))
        scale_rows[HOT, 1] = fifth[:]
        first_layer(1)
        gather_hot_bytes(2, "bytes_a")
        gather_words(2, "words_a")
        relu(0)
        relu(1)
        for j in (2, 4, 6, 8):
            first_layer(j)
            first_layer(j + 1)
            if j == 2:
                gather_hot_bytes(0, "bytes_b")
                gather_words(0, "words_b")
            if j == 8:
                quantise(6, 10)
            relu(j)
            relu(j + 1)
            turn(j - 2)
            turn(j - 1)
            square(j - 2)
            square(j - 1)
        turn(8)
        turn(9)
        square(8)
        square(9)
        second_layer(6, 10, banks[6])
        quantise(4, 6)
        second_layer(4, 6, banks[7])
        nc.scalar.copy(y_all[:, 6 * C : 10 * C], banks[6][:])
        quantise(2, 4)
        nc.vector.tensor_copy(y_all[:, 4 * C : 6 * C], banks[7][:, 0 : 2 * C])
        second_layer(2, 4, banks[4])
        quantise(0, 1)
        nc.scalar.copy(y_all[:, 2 * C : 4 * C], banks[4][:, 0 : 2 * C])
        quantise(1, 2)
        second_layer(0, 1, banks[5])
        nc.scalar.copy(y_all[:, 0:C], banks[5][:, 0:C])
        second_layer(1, 2, banks[0])
        nc.vector.tensor_copy(y_all[:, C : 2 * C], banks[0][:, 0:C])

        pieces = list(zip(CUTS, CUTS[1:]))
        fetched = {u: kept(f"fetched{u}", [P, 2, b - a], F32) for u, (a, b) in enumerate(pieces) if u > 0}
        parts = [kept(f"parts{u}", [P, 2, b - a], F32) for u, (a, b) in enumerate(pieces)]
        total = [kept(f"total{u}", [P, b - a], F32) for u, (a, b) in enumerate(pieces)]

        def picked(u, r):
            a, b = pieces[u]
            return y_all[:].indirect(pos_t[r][:, a // 16 : b // 16])

        def finish(u):
            a, b = pieces[u]
            nc.vector.tensor_tensor(total[u][:], parts[u][:, 0, :], parts[u][:, 1, :], ALU.add)
            nc.sync.dma_start(out[:, a:b], total[u][:])

        def weigh(u):
            a, b = pieces[u]
            nc.vector.tensor_tensor(parts[u][:], fetched[u][:], gates[:, :, a:b], ALU.mult)

        for r in range(2):
            nc.vector.tensor_tensor(parts[0][:, r, :], picked(0, r), gates[:, r, CUTS[0] : CUTS[1]], ALU.mult)
        for u in (1, 2):
            for r in range(2):
                nc.scalar.activation(fetched[u][:, r, :], picked(u, r), ACT.Copy)
        weigh(1)
        finish(0)
        weigh(2)
        finish(1)
        finish(2)
